import numpy as np, ml_dtypes
CORES = [3,11,19,27,35,43,51,59]
N = 8
BF = ml_dtypes.bfloat16
def gentries(a):
    return np.ascontiguousarray(a.reshape(8, 16, -1).transpose(0, 2, 1)).reshape(8, -1)
def gtable(e):
    e = np.asarray(e); return np.ascontiguousarray(e.reshape(8, -1, 16).transpose(0, 2, 1)).reshape(128, -1).astype(np.int32)
C, I, P, R, S, VM, DM = 1536, 256, 12, 5, 4, 80, 14361600
V, W, B = 2 * C, 2 * C + I, I // S
def walk(nx):
    lead = nx.shape[:-1]; full = np.concatenate([nx, np.broadcast_to(V + np.arange(I), lead + (I,))], axis=-1)
    q = [np.broadcast_to(np.arange(I), lead + (I,))]
    for k in range(1, P): q.append(np.take_along_axis(full, q[-1], -1))
    return np.stack(q, axis=-2)
def parts(rng):
    x = np.minimum((256 * rng.random((N, 8, 1, W)) * rng.random((N, 8, 16, W))).astype(np.int64), 255)
    nu = rng.integers(0, 5, (N, 8, 16)); nu[:, :, 5] = np.maximum(nu[:, :, 5], 1)
    nx = I + np.argsort(rng.random((N, 8, V)), axis=-1)
    le = rng.integers(0, 512, (N, 8, 4, C)); vol = rng.integers(1, VM + 1, (N, 8, V))
    lag = np.minimum(np.exp2(13 + 7 * rng.random((N, 8, I))).astype(np.int64), DM)
    return x, nu, nx, le, vol, lag
def pack(x, nu, nx, le, vol, lag):
    return {"x": np.ascontiguousarray(x.reshape(N, 128, W)).astype(np.float32).astype(BF), "nu": np.ascontiguousarray(nu.reshape(N, 128, 1)).astype(np.int32),
            "nx": np.stack([gtable(a) for a in nx]), "le": np.stack([gtable(a.reshape(8, -1)) for a in le]),
            "vol": np.stack([gtable(a) for a in vol]), "lag": np.stack([gtable(a) for a in lag])}
def chains(rng, lens, out, fix, own=()):
    own = np.array(own, np.int64); pool = I + rng.permutation(V - I); pool = pool[~np.isin(pool, own)]; end = np.add.accumulate(lens - 1)
    for i, p in fix:
        e = int(end[i]) - 1; j = int(np.nonzero(pool == p)[0][0]); pool[j] = pool[e]; pool[e] = p
    nx = np.zeros(V, np.int64); nx[own] = own
    for i in range(I):
        s = np.concatenate([[i], pool[end[i] - lens[i] + 1:end[i]], [V + out[i]]]).astype(np.int64); nx[s[:-1]] = s[1:]
    rest = pool[end[-1]:]; nx[rest] = rest[rng.permutation(len(rest))]
    return nx
def setup_inputs(rng):
    return pack(*parts(rng))
def setup_inputs_spread(rng):
    x, nu, nx, le, vol, lag = parts(rng)
    x = np.minimum((np.exp2(8 * rng.random((N, 8, 1, W))) * rng.random((N, 8, 16, W))).astype(np.int64), 255)
    nu = rng.choice(np.array([0, 0, 1, 4]), (N, 8, 16)); nu[:, :, 3] = 4
    le = np.minimum(np.exp2(9 * rng.random((N, 8, 4, C))).astype(np.int64) - 1, 511)
    vol = np.maximum(np.minimum(np.power(float(VM), rng.random((N, 8, V))).astype(np.int64), VM), 1)
    lag = np.maximum(np.minimum(np.power(float(DM), rng.random((N, 8, I))).astype(np.int64), DM), 1)
    return pack(x, nu, nx, le, vol, lag)
def setup_inputs_ends(rng):
    A = np.array([0, 1, I // 2, I - 2, I - 1]); D = np.array([2, 3, I // 2 + 1, I - 4, I - 3])
    o = np.setdiff1d(np.arange(I), np.concatenate([A, D])); row = np.arange(16)[:, None]
    kind = rng.choice(4, (N, 8, 1, W), p=[0.35, 0.15, 0.25, 0.25]); lane = rng.integers(0, 16, (N, 8, 1, W))
    x = np.where(kind == 0, 255, np.where(kind == 1, np.where(row == lane, 254, 255), np.where(kind == 2, 0, 255 * rng.integers(0, 2, (N, 8, 16, W)))))
    nu = 4 * rng.integers(0, 2, (N, 8, 16)); nu[:, :, 0] = 4; nu[:, 0] = 4; nu[:, 7] = 4; nu[:, 1] = 0; nu[:, 2] = 4; nu[:, 2, 15] = 0
    hi = np.array([511, 511, 510, 510])[:, None]; u = rng.random((N, 8, 1, C))
    le = np.where(u < 0.1, hi, np.where(u < 0.2, hi[::-1], np.where(u < 0.3, 511, 511 * rng.integers(0, 2, (N, 8, 4, C)))))
    vol = np.where(rng.random((N, 8, V)) < 0.5, 1, VM); lag = np.where(rng.random((N, 8, I)) < 0.5, 1, DM); nx = np.zeros((N, 8, V), np.int64)
    for r in range(N):
        for g in range(8):
            lens = np.zeros(I, np.int64); lens[A] = P; lens[D] = R + 1; lens[o] = rng.permutation(np.resize(np.array([1, P // 2, P - 1, P, P + 1]), len(o)))
            out = np.zeros(I, np.int64); out[A] = D; out[D] = A; out[o] = rng.permutation(o)
            nx[r, g] = chains(rng, lens, out, [(0, I), (1, I + 1), (I - 2, V - 2), (I - 1, V - 1)])
            q = walk(nx[r, g]); a = q[:, A]; d = q[:R + 1, D]; both = np.concatenate([a.reshape(-1), d.reshape(-1)])
            le[r, g][:, both % C] = 511
            x[r, g][:, both] = 255; x[r, g][:, V + A] = 255; x[r, g][:, V + D] = 255
            mix = 255 * rng.integers(0, 2, (16, 5)); mix[0] = 255; mix[15] = 0; x[r, g][:, d[1]] = mix
            vol[r, g, a] = VM; vol[r, g, a[1, 1]] = VM - 1
            vol[r, g, a[1:, 2:4]] = np.where(rng.random((P - 1, 2)) < 0.5, 1, VM); vol[r, g, a[1, 2:4]] = 1
            tot = 255 * int(np.sum(nu[r, g])) * np.sum(vol[r, g, a[1:]], axis=0)
            lag[r, g, D] = 1; lag[r, g, A] = DM; lag[r, g, A[2]] = max(int(tot[2]), 1); lag[r, g, A[3]] = min(max(int(tot[3]) + 1, 1), DM)
    return pack(x, nu, nx, le, vol, lag)
def setup_inputs_corners(rng):
    x, nu, nx, le, vol, lag = parts(rng); ar = np.arange(I); m = V // I
    vol = rng.choice(np.array([1, 2, VM - 1, VM]), (N, 8, V)); stay = np.array([0, 511, 511, 0])[:, None]
    for r in range(N):
        for g in range(8):
            t = (g + r) % 8; lens = None
            if t == 0: le[r, g] = stay; lens = rng.permutation(np.resize(np.array([1, 2, P - 1, P, P + 1]), I))
            if t == 1: le[r, g] = 511 - stay
            if t == 2: le[r, g] = 0; lens = np.ones(I, np.int64); lens[rng.integers(0, I)] = V - I + 1
            if t == 3: le[r, g] = stay; lens = rng.permutation(np.resize(np.array([1, P - 1]), I))
            if t == 4: le[r, g] = 511; lens = rng.permutation(np.resize(np.array([m - 1, m + 1]), I))
            if t == 5: lag[r, g] = DM; vol[r, g] = 1
            if t == 6: lag[r, g] = 1; vol[r, g] = VM; nu[r, g] = 0; nu[r, g, rng.integers(0, 16)] = 4
            if t == 7:
                e = rng.integers(-100, 101, (7, W)); nu[r, g] = 4; nu[r, g, 0] = 1
                x[r, g, 0] = 128 + rng.integers(0, 2, W); x[r, g, 1:15:2] = 100 + e; x[r, g, 2:15:2] = 100 - e; x[r, g, 15] = 100
                le[r, g] = np.array([511, 511, 510, 510])[:, None]
            if lens is not None:
                nx[r, g] = chains(rng, lens, rng.permutation(I), []); q = walk(nx[r, g])
                if t == 3:
                    off = np.ones(W, bool); off[q.reshape(-1)] = False; p = np.nonzero(off[:V])[0]; nx[r, g, p] = p
                c = np.sum(nu[r, g][:, None] * x[r, g], axis=0); c[:V] = c[:V] * vol[r, g]; c[V:] = 0
                T = np.add.accumulate(c[q], axis=0); k = rng.integers(1, P, I); j = (rng.random(I) * k).astype(np.int64)
                lag[r, g] = np.maximum(np.minimum(T[k, ar] - T[j, ar] + rng.choice(np.array([0, 0, 0, 1]), I), DM), 1)
    return pack(x, nu, nx, le, vol, lag)
def setup_inputs_calm(rng):
    x, nu, nx, le, vol, lag = parts(rng)
    x = (np.argsort(rng.random((N, 8, 16, W)), axis=2) < rng.integers(0, 4, (N, 8, 1, W))).astype(np.int64)
    nu = rng.integers(0, 3, (N, 8, 16)); nu[:, ::2] = 1; nu[:, :, 7] = 1
    le = rng.integers(0, 4, (N, 8, 4, C)); vol = rng.integers(1, 3, (N, 8, V)); vol[:, 0] = 1; vol[:, 5] = 1
    lag = rng.integers(1, 7, (N, 8, I)); t = (np.arange(N)[:, None] + np.arange(8)[None, :]) % 4
    lag = np.where(t[:, :, None] < 3, t[:, :, None] + 1, lag)
    return pack(x, nu, nx, le, vol, lag)
def setup_inputs_fine(rng):
    x, nu, nx, le, vol, lag = parts(rng); ar = np.arange(I); stay = np.array([0, 511, 511, 0])[:, None]; turn = int(rng.integers(0, 4))
    forms = np.array([[255] * 16, [255] * 13 + [182, 0, 0], [255] * 8 + [0] * 8])
    pats = np.array([[511, 511, 510, 511], [511, 510, 511, 511], [511, 511, 505, 504], [504, 505, 511, 511], [510, 509, 511, 511], [511, 511, 509, 510]]).T
    for g in range(8):
        t = (g + turn) % 4; lane = int(rng.integers(0, 16)); others = np.delete(np.arange(16), lane); nu[:, g] = 4
        if t == 0 or t == 2: nu[:, g, lane] = 1
        far = np.append(rng.permutation(I - 1)[:I // 2 - 1], I - 1); near = np.setdiff1d(ar, far); n = len(far)
        for r in range(N):
            if t == 0 or t == 2: x[r, g][others] = 255 - np.argsort(rng.random((15, W)), axis=0)
            if t == 0:
                x[r, g, lane] = 255; le[r, g] = stay; vol[r, g] = rng.integers(VM - 3, VM + 1, V)
                c = np.zeros(W, np.int64); c[:V] = 15135 * vol[r, g]; q = walk(nx[r, g]); T = np.add.accumulate(c[q], axis=0)
                k = np.maximum(np.argmax(rng.random((P, I)) * ((T >= 2 ** 23) & (q < V)), axis=0), 1); j = np.maximum(k - 1 - rng.integers(0, 3, I), 0)
                lag[r, g] = np.maximum(np.minimum(T[k, ar] - T[j, ar] + rng.integers(0, 2, I), DM), 1)
            if t == 1:
                lens = rng.integers(1, 4, I); lens[far] = P; out = np.zeros(I, np.int64); out[far] = rng.permutation(far); out[near] = rng.permutation(near)
                nx[r, g] = chains(rng, lens, out, [], C + far); a = walk(nx[r, g])[:, far]
                le[r, g] = stay; le[r, g][:, far] = np.array([0, 0, 511, 511])[:, None]
                x[r, g][:, a[1:].reshape(-1)] = 255; x[r, g][:, far] = rng.integers(100, 255, (16, n)); x[r, g][:, C + far] = rng.integers(100, 255, (16, n))
                x[r, g][:, V + far] = rng.integers(0, 61, (16, n)); vol[r, g, a[1:]] = VM
                less = rng.random(n) < 0.5; less[0] = True; e = a[rng.integers(1, P, n), np.arange(n)]; x[r, g][rng.integers(0, 16, n)[less], e[less]] = 254
                c = 4 * np.sum(x[r, g], axis=0); tot = VM * np.sum(c[a[1:]], axis=0); u = rng.random(n); u[0] = 0
                lag[r, g, far] = np.where(u < 0.5, DM, np.minimum(tot + (u < 0.75), DM))
            if t == 2:
                x[r, g, lane] = 254 + rng.integers(0, 2, W); a = rng.integers(501, 512, C); b = rng.integers(501, 512, C)
                le[r, g] = np.where(rng.random(C) < 0.5, np.stack([a, b, a - 1, b - 1]), np.stack([a - 1, b - 1, a, b]))
            if t == 3:
                z = rng.choice(3, W, p=[0.45, 0.3, 0.25]); x[r, g] = np.take_along_axis(forms[z].T, np.argsort(rng.random((16, W)), axis=0), 0)
                le[r, g] = pats[:, rng.integers(0, 6, C)]; shut = I + rng.permutation(C - I)[:(C - I) // 4]; le[r, g][:, shut] = np.array([511, 511, 0, 0])[:, None]
                both = np.concatenate([shut, C + shut]); nx[r, g, np.setdiff1d(np.arange(V), both)] = rng.permutation(np.setdiff1d(I + np.arange(V), both))
                sw = rng.random(len(shut)) < 0.5; nx[r, g, shut] = np.where(sw, C + shut, shut); nx[r, g, C + shut] = np.where(sw, shut, C + shut)
    return pack(x, nu, nx, le, vol, lag)
def check_inputs(d):
    bad = []
    for k, lo, hi in (("x", 0, 255), ("nu", 0, 4), ("nx", I, W - 1), ("le", 0, 511), ("vol", 1, VM), ("lag", 1, DM)):
        v = np.asarray(d[k]).astype(np.float64)
        if not bool(np.all((v >= lo) & (v <= hi))): bad.append("range of " + k)
    v = np.asarray(d["x"]).astype(np.float64)
    if not bool(np.all(v == np.floor(v))): bad.append("whole numbers of x")
    if not all(bool(np.all(np.sort(gentries(a), axis=1) == np.arange(I, W))) for a in d["nx"]): bad.append("nx: each number once in each group")
    return bad
def reference(x, nu, nx, le, vol, lag):
    X = x.astype(np.float32).astype(np.int64).reshape(N, 8, 16, W); w = nu.astype(np.int64).reshape(N, 8, 16, 1)
    nxt = np.stack([gentries(a) for a in nx]).astype(np.int64); ln = np.stack([gentries(a) for a in le]).astype(np.int64).reshape(N, 8, 4, C)
    vo = np.stack([gentries(a) for a in vol]).astype(np.int64); vo = np.concatenate([vo, np.zeros((N, 8, I), np.int64)], axis=2)
    de = np.stack([gentries(a) for a in lag]).astype(np.int64)
    for rnd in range(R):
        mu = np.add.reduce(w * X, axis=2)
        ex = mu.copy(); come = np.zeros((N, 8, 16, I), np.int64)
        for r in range(N):
            for s in range(S):
                ex[r, :, V + s * B:V + (s + 1) * B] = mu[(r + 1 + s) % N, :, s * B:(s + 1) * B]
                come[r, :, :, s * B:(s + 1) * B] = X[(r - 1 - s) % N, :, :, V + s * B:V + (s + 1) * B]
        m = np.take_along_axis(ex, nxt, 2); m0, m1 = m[:, :, :C], m[:, :, C:]
        cross = ln[:, :, 1] * m1 + ln[:, :, 2] * m0 < ln[:, :, 0] * m0 + ln[:, :, 3] * m1
        a, b = nxt[:, :, :C], nxt[:, :, C:]
        nxt = np.concatenate([np.where(cross, b, a), np.where(cross, a, b)], axis=2)
        q = walk(nxt)
        T = np.add.accumulate(np.take_along_axis(vo * mu, q.reshape(N, 8, P * I), 2).reshape(N, 8, P, I), axis=2)
        src = np.zeros((N, 8, P, I), np.int64) + (W + np.arange(I))
        for k in range(1, P):
            for j in range(k):
                src[:, :, k] = np.where(T[:, :, k] - T[:, :, j] >= de, q[:, :, j], src[:, :, k])
            src[:, :, k] = np.where(q[:, :, k] >= V, src[:, :, k - 1], src[:, :, k])
        new = np.take_along_axis(np.concatenate([X, come], axis=3), src.reshape(N, 8, 1, P * I), 3)
        np.put_along_axis(X, q.reshape(N, 8, 1, P * I), new, 3)
    return {"y": X.reshape(N, 128, W).astype(np.float32).astype(BF), "yn": np.stack([gtable(a) for a in nxt]).astype(np.float32)}

@@ -1,0 +1,517 @@
+from concourse.bass import DstId, RemoteDMATransfer
+from concourse.mybir import AluOpType, ActivationFunctionType
+
+NR, PL, NI, RS = 5, 12, 256, 208
+NW = 16 * RS
+BATCHES = [[_k] for _k in range(1, PL)]
+SHIFT = {"Gsnd0.1": 6000}
+MOVE = {'zVgx544.1':-1000,'Vuu128.1':-600,'aVwe512.1':3400,'aSvw256.1':1000,'aVzc0.1':3200,'Stba0.1':-1600,'aVwe256.1':600,'Pp30.15':-200,'Vuu144.1':-1900,'Vofo0.1':-1600,'Vw0.6':-200,'Vqq176.1':400,'Vcmp96.1':400,'Vuu16.1':1000,'Pp20.16':-1700,'Pp30.8':200,'aPp5156.1':1100,'aVbi0.1':-3100,'aVbi00.1':-3800,'Voff80.1':-1000,'Vtt144.1':-2500,'Pp70.7':100,'zYgx1024.1':2800,'aVwnx0.1':-1900,'Pp30.16':-1400,'Pp10.4':-500,'Vcmp576.1':400,'aVohw0.1':800,'Svg768.1':800,'Vcmp448.1':-200,'aVp10.1':-900,'aVwe384.1':600,'Vw0.9':1600,'aPp60.2':2000,'aVt10.1':2400,'Pp40.3':900,'Vtt128.1':-600,'Vcmp880.1':-800,'Vcmp48.1':600,'Pp30.17':400,'Svw1792.1':1200,'aVdab0.1':1800,'aVm340.1':500,'Vw0.7':100,'zPp60.1':3000,'Pp00.5':100,'Pp30.14':-2500,'aVzmu0.1':2400,'Vw0.5':300,'Voff128.1':-2400,'Pp20.15':-2300,'aVlagr0.1':4100,'Vtt48.1':700,'Pp30.7':-200,'aVz60.1':3200,'Vtt160.1':1600,'aVdd0.1':3300,'Vcmp240.1':-200,'Sgx1536.1':-600,'Vcmp336.1':-2000,'Vw0.8':800,'Pp70.6':300,'Vqq80.1':100,'aVoh0.1':-1000,'aGiot0.1':400,'Voff96.1':-800,'Svw2816.1':-800,'aVt20.1':-2000,'Pp10.2':300,'zVgx2592.1':3200,'Pp00.6':600,'Pp40.6':900,'Pp20.17':1500,'Vw0.2':400,'Voff144.1':-400,'Vuu112.1':100,'Vtt112.1':-400,'aVwi192.1':-1600,'Vqq64.1':200}
+XCH = [("V", 0, 36), ("S", 36, 64), ("V", 64, 100), ("S", 100, 128), ("V", 128, 162), ("S", 162, 192)]
+XPE = [(0, 64), (64, 128), (128, 192)]
+YCH = [("S", 0, 34), ("V", 34, 64), ("S", 64, 98), ("V", 98, 128), ("S", 128, 162), ("V", 162, 192)]
+XQ = 4
+MOVE = {'Ypool0.1':1000,'Vw0.8':1300,'Sw3328.1':2800,'zVofy64.1':2000,'Pp60.2':2100,'Vcmp336.1':200,'Vqq32.1':200,'Vtt96.1':-500,'Vcmp448.1':300,'zVofy128.1':1500,'Vcmp160.1':200,'Vuu96.1':-400,'zYgx2592.1':-1600,'Vuu176.1':-1100,'Vtt144.1':-1000,'Pp30.8':400,'Pp416.1':1500,'Vcmp880.1':-1200,'zYgx1568.1':1300,'Vuu144.1':-800,'aVw0.1':-4600,'aVwe0.1':1500,'aVwe128.1':1500,'aVwe256.1':1500,'aVwe384.1':1300,'aSmh0.1':1100,'aVz50.1':3000,'aVpm0.1':3300,'aVohw0.1':2700,'aVlagr0.1':3200,'aVt10.1':4800,'aVbi00.1':3100,'aVzmu0.1':2800,'aVwo0.1':-3400,'aVznx0.1':3800,'aVwc192.1':3700,'aVzn40.1':-5000,'aVp00.1':2000,'aVnuf0.1':-400,'aVwmu0.1':2500,'aVwnx0.1':-400,'aVp1192.1':3300,'aVdl0.1':2200,'aVc2192.1':2800,'aPp60.2':1400,'aVwi192.1':-400,'aVi2560.1':-2300,'aVss0.1':1700,'aVwc30.1':-800,'aVlab0.1':1600}
+PERIOD = 1550
+PLAN = {"g": 0, "n": 600, "c": 1130, "q": 1300, "u": 1900, "t": 2030, "m": 1970, "k": 3200, "o": 3990, "v": 4900, "s": 6100}
+NDMA = 72
+PIECE, SCW, SPLIT = 8, 16, "S"
+
+BF, F32, I32, U16 = "bfloat16", "float32", "int32", "uint16"
+SCRATCH = {}
+for _n, _w, _d in [
+        ("pool", NW + NR * NI, BF), ("wa", NW + NI, BF), ("wb", NW + NI, BF), ("vw", 13 * NI, BF), ("vg", 11 * NI, BF),
+        ("gx", 3072, BF), ("snd", 4 * NI, BF), ("tba", NI, BF), ("tbe", NI, BF),
+        ("nui", 1, I32), ("nxi", 192, I32), ("lei", 384, I32), ("voli", 192, I32), ("lagi", 16, I32),
+        ("pci", 1, I32), ("pmi", 1, I32), ("gci", 1, I32), ("nii", 192, I32), ("nci", 192, I32),
+        ("iot", RS, F32), ("iob", 64, F32), ("pc", 1, F32), ("pm", 1, F32), ("gc15", 1, F32), ("nuf", 1, F32),
+        ("oh", 16, F32), ("wnx", 1, F32), ("wmu", 1, F32), ("wo", 1, F32), ("wn4", 1, F32), ("bi0", 18, F32), ("bi", 18, F32),
+        ("znx", 144, BF), ("zmu", 144, BF), ("zvol", 144, BF), ("zo", 144, BF), ("zw", 144, BF), ("z1", 144, BF),
+        ("zn4", 144, BF), ("z5", 144, BF), ("z6", 144, BF), ("m34", 128, BF), ("we", 5 * 128, BF), ("i256", 128, BF),
+        ("ka", NI, BF), ("kb", NI, BF), ("base", 64, BF), ("pmu", 12, U16), ("lagr", 64, F32),
+        ("lab", 192, F32), ("dl", 96, F32), ("i1", 128, BF), ("wi", RS, BF), ("wc", RS, BF), ("volw", RS, BF),
+        ("ohw", RS, BF), ("olw", RS, BF), ("mh", RS, BF), ("ml", RS, BF),
+        ("t1", 192, F32), ("t2", 192, F32), ("t3", 192, F32), ("t4", 192, F32), ("nxe", 192, U16),
+        ("dab", 192, F32), ("dd", 96, F32), ("ab", 192, F32), ("pp", 192, F32), ("ss", 96, F32), ("ee", 96, F32),
+        ("dn", 96, F32), ("ynb", 192, F32), ("q1a", 16, F32), ("q1b", 16, F32),
+        ("qq", 32 * PL + 64, U16), ("ofo", 16, U16), ("ofy", 192, U16),
+        ("voln", 192, F32), ("cn", 192, F32), ("dcn", 96, F32), ("c0", RS, BF), ("c1", RS, BF), ("c2", RS, BF),
+        ("wc3", 1, F32), ("zc", 144, BF), ("tt", 16 * PL, F32), ("uu", 16 * PL, F32), ("cmp", 16 * 66, BF)]:
+    SCRATCH[_n] = ("sbuf", [128, _w], _d)
+SCRATCH["msg"] = ("sbuf", [128, 4, 72], BF)
+SCRATCH["rcv"] = ("sbuf", [128, 4, 72], BF)
+for _b in range(8):
+    SCRATCH["p%d" % _b] = ("psum", [128, 512], F32)
+SEMAPHORES = ["cV", "cS", "cP", "cG", "rl"] + ["ar%d" % _k for _k in range(6)] + ["d%d" % _k for _k in range(NDMA)]
+
+A = AluOpType
+COPY, IDENT = ActivationFunctionType.Copy, ActivationFunctionType.Identity
+CY, PCY, GA, SC, WAKE, WAKE0 = 1.04, 0.52, 1.56, 3.8, 120.0, 60.0
+
+
+def overlap(a, b):
+    return a[0] == b[0] and a[2] < b[3] and b[2] < a[3] and (a[1] is None or b[1] is None or a[1] == b[1])
+
+
+def build(g, core, T, topo):
+    rank = T.rank_of(core)
+    n = len(T.cores)
+    ops = []
+    phase, seen, hint = ["a"], {}, [None]
+    q = {"V": g.vector, "S": g.scalar, "P": g.tensor, "G": g, "Y": g.sync}
+
+    def R(name, lo=0, hi=1 << 20, row=None):
+        return (name, row, lo, hi)
+
+    def add(eng, fn, rd, wr, dur, kind="c", lat=0.0, tok=None, after=None):
+        ex = [R(r[0]) for r in rd + wr if len(r[0]) == 2 and r[0][0] == "p" and r[0][1].isdigit()]
+        r0 = (wr + rd)[0]
+        tag = "%s%s%s%d" % (phase[0], eng, {"wa": "w", "wb": "w"}.get(r0[0], r0[0]), r0[2] % NI if r0[0] in ("snd", "pool") else r0[2])
+        seen[tag] = seen.get(tag, 0) + 1
+        ops.append({"eng": eng, "fn": fn, "rd": rd, "wr": wr, "ex": ex, "dur": dur, "kind": kind, "lat": lat,
+                    "tok": tok, "after": after, "hint": hint[0], "tag": "%s.%d" % (tag, seen[tag])})
+        return len(ops) - 1
+
+    def vd(nel, c=1.0):
+        return max(64.0, nel * c) * CY
+
+    def ap(r, step=None):
+        name, row, lo, hi = r
+        return T[name][:, lo:hi] if step is None else T[name][:, lo:hi:step]
+
+    def ps(r):
+        return len(r[0]) == 2 and r[0][0] == "p" and r[0][1].isdigit()
+
+    def tt(o, a, b, op):
+        add("V", lambda: g.vector.tensor_tensor(ap(o), ap(a), ap(b), op), [a, b], [o], vd(o[3] - o[2], 1 if ps(a) or ps(b) else 2))
+
+    def ts(o, a, s1, s2, op0, op1=None):
+        rd = [a] + [s for s in (s1, s2) if isinstance(s, tuple)]
+        c1 = ap(s1) if isinstance(s1, tuple) else s1
+        c2 = ap(s2) if isinstance(s2, tuple) else s2
+        if op1 is None:
+            add("V", lambda: g.vector.tensor_scalar(ap(o), ap(a), c1, None, op0), rd, [o], vd(o[3] - o[2]))
+        else:
+            add("V", lambda: g.vector.tensor_scalar(ap(o), ap(a), c1, c2, op0, op1), rd, [o], vd(o[3] - o[2]))
+
+    def cp(eng, o, a):
+        if eng == "V":
+            add("V", lambda: g.vector.tensor_copy(ap(o), ap(a)), [a], [o], vd(o[3] - o[2]))
+        else:
+            add("S", lambda: g.scalar.activation(ap(o), ap(a), COPY), [a], [o], vd(o[3] - o[2]))
+
+    def gather(eng, o, win, off):
+        d = 60 + (o[3] - o[2]) * GA * CY
+        if eng == "V":
+            add("V", lambda: g.vector.tensor_copy(ap(o), ap(win).indirect(ap(off))), [win, off], [o], d)
+        else:
+            add("S", lambda: g.scalar.activation(ap(o), ap(win).indirect(ap(off)), COPY), [win, off], [o], d)
+
+    def mm(items, rd, wr):
+        def fn():
+            ins = None
+            for o, l, r, c, st, sp in items:
+                ins = g.tensor.matmul(o, l, r, st, sp)
+            return ins
+        add("P", fn, rd, wr, sum(max(64, it[3]) for it in items) * PCY, "c", 60.0)
+
+    def unwrap(bank, olo, z, src, fn_rhs, cols, piece=16):
+        o = T[bank][:, olo:olo + cols]
+        for j0 in range(0, 16, piece):
+            mm([(o, T[z][:, 15 - j:143 - j], fn_rhs(j), cols, j == 0, j == 15) for j in range(j0, j0 + piece)],
+               [R(z), src], [R(bank, olo, olo + cols)])
+
+    nd = [0]
+
+    def dma(eng, out, in_, rd, wr, nbytes):
+        s = "d%d" % nd[0]
+        nd[0] += 1
+        add(eng, lambda: q[eng].dma_start(out, in_), rd, wr, 60.0, "d", 1900.0 + nbytes / 200.0, (s, 16))
+
+    def torow(w, row, src, eng="Y"):
+        dma(eng, T[w][row:128:16, 0:NW], T[src][:, :], [R(src)], [R(w, 0, NW, row)], 53248)
+
+    nrl, sends = [0], []
+
+    def send(k, srcs, dsts, peers, rd, wr):
+        trs = []
+        for s in range(4):
+            peer = T.cores[peers[s]]
+            eng = topo.engines(core, peer)
+            per = len(eng) // 4
+            mask = sum(1 << e for e in eng[per * s:per * s + per])
+            rid, pid, _ = topo.addr(peer)
+            trs.append(RemoteDMATransfer(dst_ids=[DstId(rid=rid, pnc=pid)], dma_engine_mask=mask,
+                                         remote_sem=T.sem["ar%d" % k], src=srcs[s], dst=dsts[s]))
+            nrl[0] += per
+        i = add("G", lambda: g.remote_dma_fused(trs, local_sem=T.sem.rl), rd, [], 500.0, "r")
+        add(None, None, [], wr, 0.0, "a", 3500.0, ("ar%d" % k, 4 * per), i)
+        sends.append(i)
+
+    up = [(rank + 1 + s) % n for s in range(4)]
+    down = [(rank - 1 - s) % n for s in range(4)]
+
+    def col(name, k=0):
+        return R(name, k, k + 1)
+
+    dma("Y", T.nui[:, :], T.nu[:, :], [], [R("nui")], 512)
+    dma("Y", T.msg[:, :, 0:64], T.x[:, 0:NI], [], [R("msg", 0, 64)], 65536)
+    dma("Y", T.nxi[:, :], T.nx[:, :], [], [R("nxi")], 98304)
+    qx = NW // XQ
+    for u in range(XQ):
+        dma("S", T.pool[:, qx * u:qx * u + qx], T.x[:, qx * u:qx * u + qx], [], [R("pool", qx * u, qx * u + qx)], 256 * qx * (u + 1))
+    dma("Y", T.voli[:, :], T.vol[:, :], [], [R("voli")], 300000)
+    dma("Y", T.lei[:, :], T.le[:, :], [], [R("lei")], 500000)
+    dma("Y", T.lagi[:, :], T.lag[:, :], [], [R("lagi")], 8192)
+    add("G", lambda: g.iota(T.pci[:, :], [[0, 1]], 0, 1), [], [R("pci")], 200.0)
+    add("G", lambda: g.iota(T.iot[:, :], [[1, RS]], 0, 0, allow_small_or_imprecise_dtypes=True), [], [R("iot")], 600.0)
+    add("V", lambda: g.vector.memset(T.wa[:, :], 0.0), [], [R("wa")], vd(1792))
+    cp("V", col("nuf"), col("nui"))
+    add("V", lambda: g.vector.tensor_scalar(T.msg[:, :, 64], T.iot[:, 0:4], 0.0, T.nuf[:, 0:1], A.mult, A.add),
+        [R("iot"), R("nuf")], [R("msg", 64, 72)], vd(4))
+    send(5, [T.msg[:, s, 0:65] for s in range(4)], [T.rcv[:, s, 0:65] for s in range(4)], down, [R("msg")], [R("rcv")])
+    send(0, [T.pool[:, 3072 + 64 * s:3136 + 64 * s] for s in range(4)], [T.pool[:, NW + 64 * s:NW + 64 * s + 64] for s in range(4)],
+         up, [R("pool", 3072, NW)], [R("pool", NW, NW + NI)])
+    add("G", lambda: g.iota(T.ka[:, :], [[1, 16], [0, 16]], 0, 0, allow_small_or_imprecise_dtypes=True), [], [R("ka")], 600.0)
+    add("G", lambda: g.iota(T.kb[:, :], [[0, 16], [1, 16]], 0, 0, allow_small_or_imprecise_dtypes=True), [], [R("kb")], 600.0)
+    add("G", lambda: g.iota(T.iob[:, :], [[0, 4], [16, 16]], 0, 0, allow_small_or_imprecise_dtypes=True), [], [R("iob")], 300.0)
+    ts(col("pmi"), col("pci"), 15, None, A.bitwise_and)
+    cp("V", col("pm"), col("pmi"))
+    cp("V", col("pc"), col("pci"))
+    ts(col("gc15"), col("pc"), col("pm"), 15.0, A.subtract, A.add)
+    ts(R("zw", 0, 144), R("iot", 0, 144), col("gc15"), col("nuf"), A.is_equal, A.mult)
+    ts(R("oh", 0, 16), R("iot", 0, 16), col("pm"), None, A.is_equal)
+    ts(col("wnx"), col("oh", 0), col("oh", 1), None, A.add)
+    ts(col("wmu"), col("oh", 3), col("oh", 4), None, A.add)
+    ts(col("wo"), col("oh", 5), 16.0, col("oh", 6), A.mult, A.add)
+    ts(col("wn4"), col("oh", 4), -1.0, None, A.mult)
+    for z, w in (("zmu", col("wmu")), ("z1", 1.0), ("zn4", col("wn4")), ("znx", col("wnx")), ("zvol", col("oh", 2)),
+                 ("zo", col("wo")), ("z5", col("oh", 5)), ("z6", col("oh", 6))):
+        ts(R(z, 0, 144), R("iot", 0, 144), col("gc15"), w, A.is_equal, A.mult)
+    tt(R("m34", 0, 128), R("z1", 12, 140), R("z1", 11, 139), A.add)
+    ts(R("we", 512, 640), R("m34", 0, 128), col("nuf"), None, A.mult)
+    for s in range(4):
+        add("V", (lambda s=s: g.vector.tensor_scalar(T.we[:, 128 * s:128 * s + 128], T.m34[:, :], T.rcv[:, s, 64:65], None, A.mult)),
+            [R("m34"), R("rcv")], [R("we", 128 * s, 128 * s + 128)], vd(64))
+    ts(R("i256", 0, 128), R("iot", 0, 128), col("pc"), 256.0, A.is_equal, A.mult)
+    ts(R("base", 0, 64), R("iob", 0, 64), col("pm"), 1.0 / 256, A.add, A.mult)
+    ts(R("bi0", 0, 18), R("iot", 0, 18), -8.0, col("oh", 5), A.add, A.mult)
+    ts(R("bi", 0, 18), R("bi0", 0, 18), 16.0, None, A.mult)
+    ts(R("pmu", 0, 12), R("iot", 0, 12), 0.0, col("pm"), A.mult, A.add)
+    cp("V", R("lagr", 0, 16), R("lagi", 0, 16))
+    ts(R("ohw", 0, RS), R("iot", 0, RS), -128.0, None, A.add)
+    ts(R("olw", 0, RS), R("iot", 0, RS), 0.0, col("pm"), A.mult, A.add)
+    torow("wa", 5, "ohw")
+    torow("wa", 6, "olw")
+    add("G", lambda: g.iota(T.wb[:, :], [[0, NW + NI]], 0, 0, allow_small_or_imprecise_dtypes=True), [], [R("wb")], 7600.0,
+        after=sends[-1])
+    add("V", lambda: g.vector.memset(T.tt[:, 0:16], 0.0), [], [R("tt", 0, 16)], vd(16))
+    add("V", lambda: g.vector.memset(T.ss[:, :], 0.0), [], [R("ss")], vd(96))
+    add("V", lambda: g.vector.memset(T.volw[:, 192:RS], 0.0), [], [R("volw", 192, RS)], vd(16))
+    cp("V", R("volw", 0, 192), R("voli", 0, 192))
+    torow("wa", 2, "volw")
+    for c in ("c0", "c1", "c2"):
+        add("V", (lambda c=c: g.vector.memset(T[c][:, 192:RS], 0.0)), [], [R(c, 192, RS)], vd(16))
+    ts(col("wc3"), col("oh", 2), col("oh", 7), col("oh", 8), A.add, A.add)
+    ts(R("zc", 0, 144), R("iot", 0, 144), col("gc15"), col("wc3"), A.is_equal, A.mult)
+    ts(R("wi", 192, RS), R("olw", 0, 16), float(RS), None, A.mult)
+    cp("V", R("wc", 192, RS), R("iot", 192, RS))
+    ts(R("nii", 0, 192), R("nxi", 0, 192), 15, None, A.bitwise_and)
+    ts(R("nci", 0, 192), R("nxi", 0, 192), 4, None, A.arith_shift_right)
+    ts(R("p0", 0, 192), R("nii", 0, 192), float(RS), None, A.mult)
+    tt(R("lab", 0, 192), R("p0", 0, 192), R("nci", 0, 192), A.add)
+    ts(R("p1", 0, 192), R("nxi", 0, 192), -3071.5, 8192.0, A.add, A.mult)
+    ts(R("t2", 0, 192), R("nxi", 0, 192), 256.0, None, A.add)
+    tt(R("p1", 192, 384), R("p1", 0, 192), R("t2", 0, 192), A.min)
+    tt(R("t1", 0, 192), R("p1", 192, 384), R("lab", 0, 192), A.max)
+    cp("V", R("nxe", 0, 192), R("t1", 0, 192))
+    tt(R("dl", 0, 96), R("lab", 96, 192), R("lab", 0, 96), A.subtract)
+    tt(R("dab", 0, 192), R("lei", 0, 192), R("lei", 192, 384), A.subtract)
+    tt(R("dd", 0, 96), R("dab", 96, 192), R("dab", 0, 96), A.subtract)
+    h = RS // XQ
+    for u in range(XQ):
+        unwrap("p5", h * u, "zw", R("pool", 16 * h * u, 16 * h * (u + 1)),
+               (lambda j, u=u: T.pool[:, 16 * h * u + j:16 * h * (u + 1):16]), h)
+    cp("S", R("mh", 0, RS), R("p5", 0, RS))
+    tt(R("ml", 0, RS), R("p5", 0, RS), R("mh", 0, RS), A.subtract)
+    torow("wa", 3, "mh")
+    torow("wa", 4, "ml")
+
+    def rows(blocks, rd, tb, dst, bias):
+        mm([(T.p6[:, lo:hi], l, r, hi - lo, True, True) for lo, hi, l, r in blocks], rd + [R("we")], [R("p6", 0, NI)])
+        cp("S", R(tb, 0, NI), R("p6", 0, NI))
+        it = [(T.p7[:, 0:NI], T.zn4[:, 11:139], T[tb][:, :], NI, True, False)]
+        if bias is not None:
+            it.append((T.p7[:, 0:NI], T.z5[:, 10:138], T.ka[:, :], NI, False, False))
+            it.append((T.p7[:, 0:NI], T.z6[:, 9:137], T.kb[:, :], NI, False, False))
+        for b, (lo, hi, l, r) in enumerate(blocks):
+            it.append((T.p7[:, lo:hi], l, r, hi - lo, False, b == len(blocks) - 1))
+        mm(it, rd + [R("we"), R(tb), R("zn4"), R("z5"), R("z6"), R("ka"), R("kb")], [R("p7", 0, NI)])
+        if bias is None:
+            cp("S", dst, R("p7", 0, NI))
+        else:
+            add("S", lambda: g.scalar.activation(ap(dst), T.p7[:, 0:NI], IDENT, bias=T.bi[:, bias:bias + 1]),
+                [R("p7", 0, NI), R("bi")], [dst], vd(NI))
+
+    def weights(s):
+        return T.we[:, 128 * s:128 * s + 128]
+
+    rows([(64 * s, 64 * s + 64, weights(s), T.rcv[:, s, 0:64]) for s in range(4)], [R("rcv")], "tbe", R("wa", NW, NW + NI), None)
+    rows([(0, NI, weights(4), T.pool[:, 0:NI])], [R("pool", 0, NI)], "tba", R("vw", NI, 2 * NI), 0)
+
+    for t in range(NR):
+        wc, wn = ("wa", "wb") if t % 2 == 0 else ("wb", "wa")
+        phase[0] = ""
+        seen.clear()
+        for row in (3, 4, 5, 6):
+            if t == NR - 1 and row < 5:
+                continue
+            dma("Y", T[wn][row:128:16, 0:NW], T[wc][row:128:16, 0:NW], [R(wc, 0, NW, row)], [R(wn, 0, NW, row)], 53248)
+        for e, lo, hi in XCH:
+            gather(e, R("gx", 16 * lo, 16 * hi), R(wc, 0, NW + NI), R("nxe", lo, hi))
+        if t > 0:
+            unwrap("p0", 0, "zo", R(wc, 0, NW), (lambda j, wc=wc: T[wc][:, RS * j + 192:RS * j + RS]), 16)
+            ts(R("ofo", 0, 16), R("p0", 0, 16), 2048.0, None, A.add)
+        for lo, hi in XPE:
+            unwrap("p5", lo, "zmu", R("gx", 16 * lo, 16 * hi), (lambda j, lo=lo, hi=hi: T.gx[:, 16 * lo + j:16 * hi:16]), hi - lo)
+        if t == 0:
+            for lo, hi in XPE:
+                unwrap("p4", lo, "zvol", R("gx", 16 * lo, 16 * hi), (lambda j, lo=lo, hi=hi: T.gx[:, 16 * lo + j:16 * hi:16]), hi - lo)
+            cp("S", R("voln", 0, 192), R("p4", 0, 192))
+        tt(R("pp", 0, 96), R("p5", 0, 96), R("dab" if t == 0 else "ab", 0, 96), A.mult)
+        tt(R("p5", 384, 480), R("p5", 96, 192), R("dab" if t == 0 else "ab", 96, 192), A.mult)
+        tt(R("cn", 0, 192), R("p5", 0, 192), R("voln", 0, 192), A.mult)
+        tt(R("p5", 192, 288), R("p5", 384, 480), R("pp", 0, 96), A.subtract)
+        tt(R("p5", 288, 384), R("p5", 192, 288), R("ss", 0, 96), A.is_lt)
+        sn = R("p5", 288, 384)
+        tt(R("p5", 192, 288), sn, R("dl", 0, 96), A.mult)
+        tt(R("p1", 0, 96), R("p5", 192, 288), R("lab", 0, 96), A.add)
+        tt(R("p1", 96, 192), R("lab", 96, 192), R("p5", 192, 288), A.subtract)
+        cp(SPLIT, R("wi", 0, 192), R("p1", 0, 192))
+        tt(R("wc", 0, 192), R("p1", 0, 192), R("wi", 0, 192), A.subtract)
+        cp("V", R("qq", 32, 48), R("p1", 0, 16))
+        torow(wc, 0, "wi")
+        torow(wc, 1, "wc")
+        tt(R("dcn", 0, 96), R("cn", 96, 192), R("cn", 0, 96), A.subtract)
+        tt(R("p5", 384, 480), sn, R("dcn", 0, 96), A.mult)
+        tt(R("p2", 0, 96), R("p5", 384, 480), R("cn", 0, 96), A.add)
+        tt(R("p2", 96, 192), R("cn", 96, 192), R("p5", 384, 480), A.subtract)
+        cp(SPLIT, R("c0", 0, 192), R("p2", 0, 192))
+        tt(R("p3", 0, 192), R("p2", 0, 192), R("c0", 0, 192), A.subtract)
+        cp(SPLIT, R("c1", 0, 192), R("p3", 0, 192))
+        tt(R("c2", 0, 192), R("p3", 0, 192), R("c1", 0, 192), A.subtract)
+        torow(wc, 2, "c0")
+        torow(wc, 7, "c1", "S")
+        torow(wc, 8, "c2")
+        if t < NR - 1:
+            cp("V", R("ss", 0, 96), sn)
+            tt(R("ee", 0, 96), sn, R("dd", 0, 96), A.mult)
+            tt(R("ab", 0, 96), R("dab", 0, 96), R("ee", 0, 96), A.add)
+            tt(R("ab", 96, 192), R("dab", 96, 192), R("ee", 0, 96), A.subtract)
+        else:
+            tt(R("dn", 0, 96), R("nxi", 96, 192), R("nxi", 0, 96), A.subtract)
+            tt(R("ee", 0, 96), sn, R("dn", 0, 96), A.mult)
+            tt(R("ynb", 0, 96), R("nxi", 0, 96), R("ee", 0, 96), A.add)
+            tt(R("ynb", 96, 192), R("nxi", 96, 192), R("ee", 0, 96), A.subtract)
+            dma("Y", T.yn[:, :], T.ynb[:, :], [R("ynb")], [], 98304)
+        alo = NW + NI * t
+        if t > 0:
+            so = NI * (t - 1)
+            gather("S", R("snd", so, so + NI), R("pool", 0, alo), R("ofo", 0, 16))
+            send(t, [T.snd[:, so + 64 * s:so + 64 * s + 64] for s in range(4)],
+                 [T.pool[:, alo + 64 * s:alo + 64 * s + 64] for s in range(4)], up, [R("snd", so, so + NI)], [R("pool", alo, alo + NI)])
+            cp("S", R("vw", NI, 2 * NI), R("vw", 0, NI))
+            sb, sr = "snd", so
+        else:
+            sb, sr = "pool", 3072
+        if t < NR - 1:
+            rows([(64 * s, 64 * s + 64, weights(s), T[sb][:, sr + 64 * s:sr + 64 * s + 64]) for s in range(4)],
+                 [R(sb, sr, sr + NI)], "tbe", R(wn, NW, NW + NI), None)
+        rows([(0, NI, weights(4), T.pool[:, alo:alo + NI])], [R("pool", alo, alo + NI)], "tba", R("vw", 0, NI), 13 + t)
+        if t == NR - 1:
+            dma("Y", T.y[:, 0:NI], T.pool[:, alo:alo + NI], [R("pool", alo, alo + NI)], [], 65536)
+        co = 0
+        first = len(ops)
+        for k in range(1, PL):
+            lo, s0, s1 = NI * k, 16 * k, 16 * k + 16
+
+            def at(name, k=k, first=first):
+                hint[0] = (first + 7, (k - 2) * PERIOD + PLAN[name]) if k > 1 else None
+
+            def move(k, wn=wn, at=at):
+                vo, qi = R("vg", NI * (k - 1), NI * k), R("qq", 32 * k, 32 * k + 16)
+                at("v", k)
+                gather("S", vo, R("vw", 0, NI * (k + 1)), R("qq", 32 * k + 80, 32 * k + 96))
+                at("s", k)
+                add("V", (lambda: g.vector.tensor_copy(T[wn][:, 0:NW].indirect(ap(qi)), ap(vo))),
+                    [vo, qi], [R(wn, 0, NW)], 50 + NI * SC * CY)
+            if k > 1:
+                at("g")
+                gather("S", R("vw", lo, lo + NI), R(wc, 0, NW), R("qq", 2 * s0 - 32, 2 * s0 - 16))
+                bank, cb = "p%d" % (k % 2), "p%d" % (2 + k % 2)
+                at("n" if k < PL - 1 else "c")
+                unwrap(bank, 0, "znx", R("vw", lo, lo + NI), (lambda j, lo=lo: T.vw[:, lo + j:lo + NI:16]), 16)
+                at("q")
+                w = 32 if k > 3 else 16
+                cp("V", R("qq", 2 * s0, 2 * s0 + w), R(bank, 0, w))
+                if k > 3:
+                    move(k - 2)
+                at("c" if k < PL - 1 else "n")
+                unwrap(cb, 0, "zc", R("vw", lo, lo + NI), (lambda j, lo=lo: T.vw[:, lo + j:lo + NI:16]), 16, PIECE)
+                at("u")
+                tt(R("uu", s0, s1), R(cb, 0, 16), R("uu", s0 - 16, s0), A.add)
+                at("t")
+                if k < PL - 1:
+                    tt(R("tt", s0, s1), R(cb, 0, 16), R("tt", s0 - 16, s0), A.add)
+            else:
+                tt(R("uu", 16, 32), R("p2", 0, 16), R("lagr", 0, 16), A.subtract)
+                cp("V", R("tt", 16, 32), R("p2", 0, 16))
+            at("m")
+            add("V", (lambda k=k, co=co: g.vector.tensor_tensor(
+                T.cmp[:, co:co + 16 * k], T.uu[:, 16 * k:16 * k + 16].indirect(T.pmu[:, 0:k]), T.tt[:, 0:16 * k], A.is_ge)),
+                [R("uu", s0, s1), R("pmu"), R("tt", 0, s0)], [R("cmp", co, co + s0)], 50 + s0 * GA * CY)
+            nb = "p%d" % (k % 2) if 1 < k < PL - 2 else ("p4" if k % 2 == 1 else "p7")
+            at("k")
+            mm([(T[nb][:, 16:32], T.i256[:, :], T.base[:, 0:16], 16, True, False)]
+               + [(T[nb][:, 16:32], T.i256[:, :], T.cmp[:, co + 16 * j:co + 16 * j + 16], 16, False, j == k - 1) for j in range(k)],
+               [R("i256"), R("base"), R("cmp", co, co + s0)], [R(nb, 16, 32)])
+            co += s0
+            if not 1 < k < PL - 2:
+                at("o")
+                cp("V", R("qq", 2 * s0 + 80, 2 * s0 + 96), R(nb, 16, 32))
+                move(k)
+            hint[0] = None
+    wf = "wb" if NR % 2 == 1 else "wa"
+    phase[0] = "z"
+    for bank, lo, hi in (("p5", 0, 64), ("p6", 64, 128), ("p0", 128, 192)):
+        unwrap(bank, 0, "zo", R(wf, 0, NW), (lambda j, lo=lo, hi=hi: T[wf][:, RS * j + 16 + lo:RS * j + 16 + hi]), hi - lo)
+        ts(R("ofy", lo, hi), R(bank, 0, hi - lo), 2048.0, None, A.add)
+    for e, lo, hi in YCH:
+        gather(e, R("gx", 16 * lo, 16 * hi), R("pool", 0, NW + NR * NI), R("ofy", lo, hi))
+        dma("Y", T.y[:, NI + 16 * lo:NI + 16 * hi], T.gx[:, 16 * lo:16 * hi], [R("gx", 16 * lo, 16 * hi)], [], 4096 * (hi - lo))
+    return ops, q, nrl[0]
+
+
+def depend(ops):
+    n = len(ops)
+    dep = [dict() for _ in range(n)]
+    hist = {}
+    for i, o in enumerate(ops):
+        d = dep[i]
+        for kind, regs in (("r", o["rd"]), ("w", o["wr"]), ("x", o["ex"])):
+            for r in regs:
+                for j, k2, r2 in hist.get(r[0], []):
+                    if j == i or not overlap(r, r2):
+                        continue
+                    if kind == "r" and k2 == "w":
+                        d[j] = True
+                    elif kind == "w" and k2 != "x":
+                        d.setdefault(j, False)
+                    elif kind == "x" and k2 == "x" and (ops[j]["eng"] != o["eng"] or o["eng"] == "P"):
+                        d.setdefault(j, False)
+        for kind, regs in (("r", o["rd"]), ("w", o["wr"]), ("x", o["ex"])):
+            for r in regs:
+                hist.setdefault(r[0], []).append((i, kind, r))
+    return dep
+
+
+def order(ops, dep, shift):
+    n = len(ops)
+    succ = [[] for _ in range(n)]
+    pre = [list(dep[i]) + ([ops[i]["after"]] if ops[i]["after"] is not None else []) for i in range(n)]
+    for i in range(n):
+        for j in pre[i]:
+            succ[j].append(i)
+    prio = [0.0] * n
+    for i in range(n - 1, -1, -1):
+        prio[i] = max(1.0, ops[i]["dur"] + ops[i]["lat"] + WAKE + shift.get(ops[i]["tag"], 0)) + max([prio[j] for j in succ[i]] + [0.0])
+    fin = [0.0] * n
+    start = [0.0] * n
+    busy = {e: [] for e in ("V", "S", "P", "G", "Y")}
+    rank = sorted(range(n), key=lambda i: (-prio[i], i))
+    for i in rank:
+        t = 0.0
+        for j in pre[i]:
+            same = ops[j]["eng"] == ops[i]["eng"] and ops[j]["kind"] == "c"
+            if same and ops[i]["eng"] == "P":
+                t = max(t, start[j] + ops[j]["dur"])
+            else:
+                t = max(t, fin[j] + (WAKE0 if same else WAKE))
+        e, d = ops[i]["eng"], ops[i]["dur"]
+        if e is not None:
+            l = busy[e]
+            k = len(l)
+            while k > 0 and l[k - 1][1] > t:
+                k -= 1
+            while k < len(l) and l[k][0] < t + d:
+                t = max(t, l[k][1])
+                k += 1
+            l.insert(k, (t, t + d))
+        start[i] = t
+        fin[i] = t + d + ops[i]["lat"]
+    return start, fin, pre
+
+
+def sequence(ops, start, pre, move):
+    key = []
+    for i, o in enumerate(ops):
+        t = start[i] if o["hint"] is None else start[o["hint"][0]] + o["hint"][1]
+        key.append(max([t + move.get(o["tag"], 0)] + [key[j] + 0.001 for j in pre[i]]))
+    return sorted(range(len(ops)), key=lambda i: (key[i], i))
+
+
+def rank_program(g, core, T, topo):
+    if T.rank_of(core) is None:
+        return
+    ops, q, nrl = build(g, core, T, topo)
+    dep = depend(ops)
+    start, fin, pre = order(ops, dep, SHIFT)
+    seq = sequence(ops, start, pre, MOVE)
+    pos = {i: k for k, i in enumerate(seq)}
+    need = [[] for _ in ops]
+    for i, o in enumerate(ops):
+        if o["kind"] == "a":
+            continue
+        last = {}
+        for j, raw in dep[i].items():
+            p = ops[j]
+            if p["kind"] == "r":
+                continue
+            if p["kind"] == "c":
+                if p["eng"] == o["eng"] and o["kind"] == "c" and p["eng"] == "P":
+                    continue
+                if p["eng"] not in last or pos[j] > pos[last[p["eng"]]]:
+                    last[p["eng"]] = j
+            else:
+                need[i].append(j)
+        need[i] += list(last.values())
+    seen = {}
+    marked = set()
+    waits = [[] for _ in ops]
+    for i in seq:
+        e = ops[i]["eng"]
+        for j in need[i]:
+            key = (e, ops[j]["eng"]) if ops[j]["kind"] == "c" else (e, ops[j]["tok"][0])
+            if seen.get(key, -1) < pos[j]:
+                seen[key] = pos[j]
+                waits[i].append(j)
+                marked.add(j)
+    count = {}
+    for i in seq:
+        if ops[i]["kind"] == "c" and i in marked:
+            s = "c" + ops[i]["eng"]
+            count[s] = count.get(s, 0) + 1
+            ops[i]["tok"] = (s, count[s])
+    for i in seq:
+        o = ops[i]
+        if o["kind"] == "a":
+            continue
+        for j in waits[i]:
+            q[o["eng"]].wait_ge(T.sem[ops[j]["tok"][0]], ops[j]["tok"][1])
+        ins = o["fn"]()
+        if o["kind"] == "d":
+            ins.then_inc(T.sem[o["tok"][0]], 16)
+        elif o["kind"] == "c" and i in marked:
+            ins.then_inc(T.sem[o["tok"][0]], 1)
+    g.wait_ge(T.sem.rl, nrl)
+    for i in sorted((i for i in seq if ops[i]["kind"] in "da" and i not in marked), key=lambda i: fin[i]):
+        g.wait_ge(T.sem[ops[i]["tok"][0]], ops[i]["tok"][1])

@@ -1,41 +1,40 @@
 from concourse.bass import DstId, RemoteDMATransfer
 from concourse.mybir import AluOpType, ActivationFunctionType
 
-NR, PL, NI, RS = 5, 12, 256, 208
-NW = 16 * RS
-BATCHES = [[_k] for _k in range(1, PL)]
-SHIFT = {"Gsnd0.1": 6000}
-MOVE = {'zVgx544.1':-1000,'Vuu128.1':-600,'aVwe512.1':3400,'aSvw256.1':1000,'aVzc0.1':3200,'Stba0.1':-1600,'aVwe256.1':600,'Pp30.15':-200,'Vuu144.1':-1900,'Vofo0.1':-1600,'Vw0.6':-200,'Vqq176.1':400,'Vcmp96.1':400,'Vuu16.1':1000,'Pp20.16':-1700,'Pp30.8':200,'aPp5156.1':1100,'aVbi0.1':-3100,'aVbi00.1':-3800,'Voff80.1':-1000,'Vtt144.1':-2500,'Pp70.7':100,'zYgx1024.1':2800,'aVwnx0.1':-1900,'Pp30.16':-1400,'Pp10.4':-500,'Vcmp576.1':400,'aVohw0.1':800,'Svg768.1':800,'Vcmp448.1':-200,'aVp10.1':-900,'aVwe384.1':600,'Vw0.9':1600,'aPp60.2':2000,'aVt10.1':2400,'Pp40.3':900,'Vtt128.1':-600,'Vcmp880.1':-800,'Vcmp48.1':600,'Pp30.17':400,'Svw1792.1':1200,'aVdab0.1':1800,'aVm340.1':500,'Vw0.7':100,'zPp60.1':3000,'Pp00.5':100,'Pp30.14':-2500,'aVzmu0.1':2400,'Vw0.5':300,'Voff128.1':-2400,'Pp20.15':-2300,'aVlagr0.1':4100,'Vtt48.1':700,'Pp30.7':-200,'aVz60.1':3200,'Vtt160.1':1600,'aVdd0.1':3300,'Vcmp240.1':-200,'Sgx1536.1':-600,'Vcmp336.1':-2000,'Vw0.8':800,'Pp70.6':300,'Vqq80.1':100,'aVoh0.1':-1000,'aGiot0.1':400,'Voff96.1':-800,'Svw2816.1':-800,'aVt20.1':-2000,'Pp10.2':300,'zVgx2592.1':3200,'Pp00.6':600,'Pp40.6':900,'Pp20.17':1500,'Vw0.2':400,'Voff144.1':-400,'Vuu112.1':100,'Vtt112.1':-400,'aVwi192.1':-1600,'Vqq64.1':200}
-XCH = [("V", 0, 36), ("S", 36, 64), ("V", 64, 100), ("S", 100, 128), ("V", 128, 162), ("S", 162, 192)]
-XPE = [(0, 64), (64, 128), (128, 192)]
+NR, PL, NI, RS = 5, 12, 256, 192
+NP, NW, NC = 16 * RS, 16 * RS + NI, RS // 2
+DH, DL, VO, CH, P0, P1, P2, CL, G0, G1, G2, IH, HI, LO, HX, IL = range(16)
+ROUND16, ROUND128 = 1.5 * 2.0 ** 27, 1.5 * 2.0 ** 30
+XCH0 = [("V", 0, 34), ("S", 34, 64), ("V", 64, 98), ("S", 98, 128), ("V", 128, 162), ("S", 162, 192)]
+XCH = [("V", 0, 24), ("S", 24, 60), ("V", 60, 108), ("S", 108, 144), ("V", 144, 168), ("S", 168, 180), ("V", 180, 192)]
 YCH = [("S", 0, 34), ("V", 34, 64), ("S", 64, 98), ("V", 98, 128), ("S", 128, 162), ("V", 162, 192)]
-XQ = 4
-MOVE = {'Ypool0.1':1000,'Vw0.8':1300,'Sw3328.1':2800,'zVofy64.1':2000,'Pp60.2':2100,'Vcmp336.1':200,'Vqq32.1':200,'Vtt96.1':-500,'Vcmp448.1':300,'zVofy128.1':1500,'Vcmp160.1':200,'Vuu96.1':-400,'zYgx2592.1':-1600,'Vuu176.1':-1100,'Vtt144.1':-1000,'Pp30.8':400,'Pp416.1':1500,'Vcmp880.1':-1200,'zYgx1568.1':1300,'Vuu144.1':-800,'aVw0.1':-4600,'aVwe0.1':1500,'aVwe128.1':1500,'aVwe256.1':1500,'aVwe384.1':1300,'aSmh0.1':1100,'aVz50.1':3000,'aVpm0.1':3300,'aVohw0.1':2700,'aVlagr0.1':3200,'aVt10.1':4800,'aVbi00.1':3100,'aVzmu0.1':2800,'aVwo0.1':-3400,'aVznx0.1':3800,'aVwc192.1':3700,'aVzn40.1':-5000,'aVp00.1':2000,'aVnuf0.1':-400,'aVwmu0.1':2500,'aVwnx0.1':-400,'aVp1192.1':3300,'aVdl0.1':2200,'aVc2192.1':2800,'aPp60.2':1400,'aVwi192.1':-400,'aVi2560.1':-2300,'aVss0.1':1700,'aVwc30.1':-800,'aVlab0.1':1600}
-PERIOD = 1550
-PLAN = {"g": 0, "n": 600, "c": 1130, "q": 1300, "u": 1900, "t": 2030, "m": 1970, "k": 3200, "o": 3990, "v": 4900, "s": 6100}
-NDMA = 72
-PIECE, SCW, SPLIT = 8, 16, "S"
+XQ, MID = 4, 2048
+SHARE, VSIGN = 4, 3
+KEEP = 4
+AHEAD = 4
+APART = (2, 3, 11)
+STEP = {2: "g b w1 n q d a k1 k", 3: "g s1 n d f1 k a q", 4: "g o2 m2 s1 n f1 d k a q o1 s w2",
+        0: "g f1 n d q m2 c1 a s w2", PL - 1: "g f1 d n q m2 s w2 m1 f o m w1 w"}
+NDMA = 100
+CY, PCY, GA, SC, WAKE, DMA, REMOTE = 1.0, 0.5, 1.5, 3.5, 250.0, 1600.0, 3800.0
 
 BF, F32, I32, U16 = "bfloat16", "float32", "int32", "uint16"
 SCRATCH = {}
 for _n, _w, _d in [
-        ("pool", NW + NR * NI, BF), ("wa", NW + NI, BF), ("wb", NW + NI, BF), ("vw", 13 * NI, BF), ("vg", 11 * NI, BF),
-        ("gx", 3072, BF), ("snd", 4 * NI, BF), ("tba", NI, BF), ("tbe", NI, BF),
-        ("nui", 1, I32), ("nxi", 192, I32), ("lei", 384, I32), ("voli", 192, I32), ("lagi", 16, I32),
-        ("pci", 1, I32), ("pmi", 1, I32), ("gci", 1, I32), ("nii", 192, I32), ("nci", 192, I32),
-        ("iot", RS, F32), ("iob", 64, F32), ("pc", 1, F32), ("pm", 1, F32), ("gc15", 1, F32), ("nuf", 1, F32),
-        ("oh", 16, F32), ("wnx", 1, F32), ("wmu", 1, F32), ("wo", 1, F32), ("wn4", 1, F32), ("bi0", 18, F32), ("bi", 18, F32),
-        ("znx", 144, BF), ("zmu", 144, BF), ("zvol", 144, BF), ("zo", 144, BF), ("zw", 144, BF), ("z1", 144, BF),
-        ("zn4", 144, BF), ("z5", 144, BF), ("z6", 144, BF), ("m34", 128, BF), ("we", 5 * 128, BF), ("i256", 128, BF),
-        ("ka", NI, BF), ("kb", NI, BF), ("base", 64, BF), ("pmu", 12, U16), ("lagr", 64, F32),
-        ("lab", 192, F32), ("dl", 96, F32), ("i1", 128, BF), ("wi", RS, BF), ("wc", RS, BF), ("volw", RS, BF),
-        ("ohw", RS, BF), ("olw", RS, BF), ("mh", RS, BF), ("ml", RS, BF),
-        ("t1", 192, F32), ("t2", 192, F32), ("t3", 192, F32), ("t4", 192, F32), ("nxe", 192, U16),
-        ("dab", 192, F32), ("dd", 96, F32), ("ab", 192, F32), ("pp", 192, F32), ("ss", 96, F32), ("ee", 96, F32),
-        ("dn", 96, F32), ("ynb", 192, F32), ("q1a", 16, F32), ("q1b", 16, F32),
-        ("qq", 32 * PL + 64, U16), ("ofo", 16, U16), ("ofy", 192, U16),
-        ("voln", 192, F32), ("cn", 192, F32), ("dcn", 96, F32), ("c0", RS, BF), ("c1", RS, BF), ("c2", RS, BF),
-        ("wc3", 1, F32), ("zc", 144, BF), ("tt", 16 * PL, F32), ("uu", 16 * PL, F32), ("cmp", 16 * 66, BF)]:
+        ("pool", NW + NR * NI, BF), ("st", NW + NI, BF), ("kw", NW, BF), ("vw", PL * NI, BF), ("vg", 11 * NI, BF),
+        ("gx", NP, BF), ("snd", 4 * NI, BF), ("tba", NI, BF), ("tbe", NI, BF), ("b0", 3 * NI, BF), ("ck", NI, BF), ("sg", 11 * NI, BF),
+        ("nui", 1, I32), ("nxi", RS, I32), ("lei", 2 * RS, I32), ("voli", RS, I32), ("lagi", 16, I32),
+        ("pci", 1, I32), ("pmi", 1, I32), ("nii", RS, I32), ("nci", RS, I32),
+        ("iot", RS, F32), ("pc", 8, F32), ("nuf", 1, F32), ("oh", 16, F32), ("wt", 16, F32), ("bi", 18, F32),
+        ("zw", 144, BF), ("z1", 144, BF), ("zmu", 144, BF), ("zvol", 144, BF), ("zo", 144, BF), ("zx", 144, BF), ("zn", 144, BF),
+        ("zf", 144, BF), ("m34", 128, BF), ("we", 5 * 128, BF), ("dg", 3 * 128, BF), ("ka", NI, BF), ("kb", NI, BF),
+        ("pat", 128, BF), ("bw", 3 * 128, BF), ("zd", PL * 128, BF), ("dp", 320, BF), ("zc", 128, BF), ("fb", 48, BF),
+        ("lab", RS, F32), ("hi", RS, BF), ("lo", RS, BF), ("hx", RS, BF), ("d4", 2 * RS, BF), ("dy", 2 * RS, BF), ("dl", 16, F32),
+        ("volw", RS, BF), ("ohw", RS, BF), ("olw", RS, BF), ("mh", RS, BF), ("ml", RS, BF),
+        ("lagr", 32, F32), ("base", 32, F32), ("t1", RS, F32), ("t2", RS, F32), ("nxe", 2 * RS, U16),
+        ("dab", RS, F32), ("dd", NC, F32), ("ab", RS, F32), ("xa", NC, F32), ("df", NC, F32), ("dn", NC, F32), ("ynb", RS, F32),
+        ("q1", 64, F32), ("qq", 32 * (PL + 3), U16), ("ofy", RS, U16), ("pp", RS, F32), ("ee", NC, F32),
+        ("voln", RS, F32), ("cn", NC, F32), ("dcn", NC, F32), ("c0", RS, BF), ("c1", RS, BF), ("c2", RS, BF)]:
     SCRATCH[_n] = ("sbuf", [128, _w], _d)
 SCRATCH["msg"] = ("sbuf", [128, 4, 72], BF)
 SCRATCH["rcv"] = ("sbuf", [128, 4, 72], BF)
@@ -44,60 +43,73 @@ for _b in range(8):
 SEMAPHORES = ["cV", "cS", "cP", "cG", "rl"] + ["ar%d" % _k for _k in range(6)] + ["d%d" % _k for _k in range(NDMA)]
 
 A = AluOpType
-COPY, IDENT = ActivationFunctionType.Copy, ActivationFunctionType.Identity
-CY, PCY, GA, SC, WAKE, WAKE0 = 1.04, 0.52, 1.56, 3.8, 120.0, 60.0
+COPY, IDENT, SIGN = ActivationFunctionType.Copy, ActivationFunctionType.Identity, ActivationFunctionType.Sign
 
 
 def overlap(a, b):
-    return a[0] == b[0] and a[2] < b[3] and b[2] < a[3] and (a[1] is None or b[1] is None or a[1] == b[1])
+    return a[0] == b[0] and a[2] < b[3] and b[2] < a[3] and (a[1] is None or b[1] is None or bool(a[1] & b[1]))
+
+
+def psum(r):
+    return len(r[0]) == 2 and r[0][0] == "p" and r[0][1].isdigit()
 
 
 def build(g, core, T, topo):
     rank = T.rank_of(core)
     n = len(T.cores)
-    ops = []
-    phase, seen, hint = ["a"], {}, [None]
+    ops, fixed = [], [False]
     q = {"V": g.vector, "S": g.scalar, "P": g.tensor, "G": g, "Y": g.sync}
 
-    def R(name, lo=0, hi=1 << 20, row=None):
-        return (name, row, lo, hi)
+    def R(name, lo=0, hi=1 << 20, rows=None):
+        return (name, None if rows is None else frozenset(rows), lo, hi)
 
-    def add(eng, fn, rd, wr, dur, kind="c", lat=0.0, tok=None, after=None):
-        ex = [R(r[0]) for r in rd + wr if len(r[0]) == 2 and r[0][0] == "p" and r[0][1].isdigit()]
-        r0 = (wr + rd)[0]
-        tag = "%s%s%s%d" % (phase[0], eng, {"wa": "w", "wb": "w"}.get(r0[0], r0[0]), r0[2] % NI if r0[0] in ("snd", "pool") else r0[2])
-        seen[tag] = seen.get(tag, 0) + 1
-        ops.append({"eng": eng, "fn": fn, "rd": rd, "wr": wr, "ex": ex, "dur": dur, "kind": kind, "lat": lat,
-                    "tok": tok, "after": after, "hint": hint[0], "tag": "%s.%d" % (tag, seen[tag])})
-        return len(ops) - 1
+    def col(name, k=0):
+        return R(name, k, k + 1)
 
-    def vd(nel, c=1.0):
-        return max(64.0, nel * c) * CY
+    def add(eng, fn, rd, wr, dur, kind="c", tok=None, lat=0.0):
+        ops.append({"eng": eng, "fn": fn, "rd": rd, "wr": wr, "ex": [R(r[0]) for r in rd + wr if psum(r)], "kind": kind, "tok": tok,
+                    "dur": dur, "lat": lat, "fixed": fixed[0]})
 
-    def ap(r, step=None):
-        name, row, lo, hi = r
-        return T[name][:, lo:hi] if step is None else T[name][:, lo:hi:step]
+    def ap(r):
+        return T[r[0]][:, r[2]:r[3]]
 
-    def ps(r):
-        return len(r[0]) == 2 and r[0][0] == "p" and r[0][1].isdigit()
+    def span(o, a=None, c=1.0):
+        if a is not None and SCRATCH[o[0]][2] in (BF, U16) and SCRATCH[a[0]][2] in (BF, U16):
+            c = 0.5
+        return max(64.0, (o[3] - o[2]) * c) * CY
 
     def tt(o, a, b, op):
-        add("V", lambda: g.vector.tensor_tensor(ap(o), ap(a), ap(b), op), [a, b], [o], vd(o[3] - o[2], 1 if ps(a) or ps(b) else 2))
+        add("V", lambda: g.vector.tensor_tensor(ap(o), ap(a), ap(b), op), [a, b], [o], span(o, None, 1 if psum(a) or psum(b) else 2))
 
-    def ts(o, a, s1, s2, op0, op1=None):
+    def ts(o, a, s1, op0, s2=None, op1=None):
         rd = [a] + [s for s in (s1, s2) if isinstance(s, tuple)]
         c1 = ap(s1) if isinstance(s1, tuple) else s1
         c2 = ap(s2) if isinstance(s2, tuple) else s2
         if op1 is None:
-            add("V", lambda: g.vector.tensor_scalar(ap(o), ap(a), c1, None, op0), rd, [o], vd(o[3] - o[2]))
+            add("V", lambda: g.vector.tensor_scalar(ap(o), ap(a), c1, None, op0), rd, [o], span(o, a))
         else:
-            add("V", lambda: g.vector.tensor_scalar(ap(o), ap(a), c1, c2, op0, op1), rd, [o], vd(o[3] - o[2]))
+            add("V", lambda: g.vector.tensor_scalar(ap(o), ap(a), c1, c2, op0, op1), rd, [o], span(o, a))
 
     def cp(eng, o, a):
         if eng == "V":
-            add("V", lambda: g.vector.tensor_copy(ap(o), ap(a)), [a], [o], vd(o[3] - o[2]))
+            add("V", lambda: g.vector.tensor_copy(ap(o), ap(a)), [a], [o], span(o, a))
         else:
-            add("S", lambda: g.scalar.activation(ap(o), ap(a), COPY), [a], [o], vd(o[3] - o[2]))
+            add("S", lambda: g.scalar.activation(ap(o), ap(a), COPY), [a], [o], span(o))
+
+    def scaled(o, a, w):
+        add("S", lambda: g.scalar.activation(ap(o), ap(a), COPY, scale=ap(w)), [a, w], [o], span(o))
+
+    def shifted(o, a, b, func=IDENT):
+        add("S", lambda: g.scalar.activation(ap(o), ap(a), func, bias=ap(b)), [a, b], [o], span(o))
+
+    def fill(o, v=0.0):
+        add("V", lambda: g.vector.memset(ap(o), v), [], [o], span(o, o))
+
+    def iota(o, pattern):
+        add("G", lambda: g.iota(ap(o), pattern, 0, 0, allow_small_or_imprecise_dtypes=True), [], [o], 130 + 2 * span(o))
+
+    def select(o, a, pattern, base, by_row=0):
+        add("G", lambda: g.affine_select(ap(o), ap(a), pattern, A.is_ge, 0.0, base, by_row), [a], [o], 170 + 2 * span(o))
 
     def gather(eng, o, win, off):
         d = 60 + (o[3] - o[2]) * GA * CY
@@ -109,28 +121,33 @@ def build(g, core, T, topo):
     def mm(items, rd, wr):
         def fn():
             ins = None
-            for o, l, r, c, st, sp in items:
+            for o, l, r, st, sp in items:
                 ins = g.tensor.matmul(o, l, r, st, sp)
             return ins
-        add("P", fn, rd, wr, sum(max(64, it[3]) for it in items) * PCY, "c", 60.0)
+        add("P", fn, rd, wr, sum(it[0].shape[1] for it in items) * PCY)
 
-    def unwrap(bank, olo, z, src, fn_rhs, cols, piece=16):
-        o = T[bank][:, olo:olo + cols]
-        for j0 in range(0, 16, piece):
-            mm([(o, T[z][:, 15 - j:143 - j], fn_rhs(j), cols, j == 0, j == 15) for j in range(j0, j0 + piece)],
-               [R(z), src], [R(bank, olo, olo + cols)])
+    def unwrap(o, z, src, rhs, j0=0, j1=16, first=()):
+        mm([(ap(o), ap(sq("dg", 0)), ap(f), x == 0, False) for x, f in enumerate(first)]
+           + [(ap(o), T[z][:, 15 - j:143 - j], rhs(j), j == 0 and not first, j == 15) for j in range(j0, j1)],
+           [R(z), src] + list(first) + ([sq("dg", 0)] if first else []), [o])
+
+    def unwrap16(o, z, src, first=()):
+        unwrap(o, z, src, lambda j: T[src[0]][:, src[2] + j:src[3]:16], 0, 16, first)
+
+    def sq(name, k):
+        return R(name, 128 * k, 128 * k + 128)
 
     nd = [0]
 
-    def dma(eng, out, in_, rd, wr, nbytes):
+    def dma(eng, out, in_, rd, wr, lat=DMA):
         s = "d%d" % nd[0]
         nd[0] += 1
-        add(eng, lambda: q[eng].dma_start(out, in_), rd, wr, 60.0, "d", 1900.0 + nbytes / 200.0, (s, 16))
+        add(eng, lambda: q[eng].dma_start(out, in_), rd, wr, 60.0, "d", (s, 16), lat)
 
     def torow(w, row, src, eng="Y"):
-        dma(eng, T[w][row:128:16, 0:NW], T[src][:, :], [R(src)], [R(w, 0, NW, row)], 53248)
+        dma(eng, T[w][row:128:16, 0:NP], ap(src), [src], [R(w, 0, NP, [row])])
 
-    nrl, sends = [0], []
+    nrl = [0]
 
     def send(k, srcs, dsts, peers, rd, wr):
         trs = []
@@ -143,299 +160,363 @@ def build(g, core, T, topo):
             trs.append(RemoteDMATransfer(dst_ids=[DstId(rid=rid, pnc=pid)], dma_engine_mask=mask,
                                          remote_sem=T.sem["ar%d" % k], src=srcs[s], dst=dsts[s]))
             nrl[0] += per
-        i = add("G", lambda: g.remote_dma_fused(trs, local_sem=T.sem.rl), rd, [], 500.0, "r")
-        add(None, None, [], wr, 0.0, "a", 3500.0, ("ar%d" % k, 4 * per), i)
-        sends.append(i)
+        add("G", lambda: g.remote_dma_fused(trs, local_sem=T.sem.rl), rd, [], 500.0, "r")
+        add(None, None, [], wr, 0.0, "a", ("ar%d" % k, 4 * per), REMOTE)
 
     up = [(rank + 1 + s) % n for s in range(4)]
     down = [(rank - 1 - s) % n for s in range(4)]
+    full = lambda name: R(name, 0, RS)
+    ha = lambda name, lo=0: R(name, lo, lo + NC)
+    hb = lambda name, lo=0: R(name, lo + NC, lo + RS)
+    blk = lambda name, k: R(name, NI * k, NI * k + NI)
+    pc, pm, gc15, gi, half, pr = [col("pc", k) for k in range(6)]
+    oh = lambda k: col("oh", k)
+    wt = lambda k: col("wt", k)
 
-    def col(name, k=0):
-        return R(name, k, k + 1)
+    def rows(bank, blocks, rd, tb, dst, bias):
+        o = R(bank, 0, NI)
+        it = [] if bias is None else [(ap(o), ap(sq("dg", 1)), T.ka[:, :], True, False), (ap(o), ap(sq("dg", 2)), T.kb[:, :], False, not blocks)]
+        if it:
+            mm(it, [R("dg", 128, 384), R("ka"), R("kb")], [o])
+        if blocks:
+            mm([(T[bank][:, lo:hi], l, r, bias is None, True) for lo, hi, l, r in blocks], rd, [o])
+        b = col("bi", bias or 0)
+        if blocks:
+            add("S", lambda: g.scalar.activation(T[tb][:, :], ap(o), IDENT, bias=ap(b), scale=ap(oh(CL))), [o, b, oh(CL)], [R(tb)], span(o))
+            tt(dst, o, R(tb, 0, NI), A.subtract)
+        else:
+            ts(dst, o, b, A.subtract)
 
-    dma("Y", T.nui[:, :], T.nu[:, :], [], [R("nui")], 512)
-    dma("Y", T.msg[:, :, 0:64], T.x[:, 0:NI], [], [R("msg", 0, 64)], 65536)
-    dma("Y", T.nxi[:, :], T.nx[:, :], [], [R("nxi")], 98304)
-    qx = NW // XQ
-    for u in range(XQ):
-        dma("S", T.pool[:, qx * u:qx * u + qx], T.x[:, qx * u:qx * u + qx], [], [R("pool", qx * u, qx * u + qx)], 256 * qx * (u + 1))
-    dma("Y", T.voli[:, :], T.vol[:, :], [], [R("voli")], 300000)
-    dma("Y", T.lei[:, :], T.le[:, :], [], [R("lei")], 500000)
-    dma("Y", T.lagi[:, :], T.lag[:, :], [], [R("lagi")], 8192)
-    add("G", lambda: g.iota(T.pci[:, :], [[0, 1]], 0, 1), [], [R("pci")], 200.0)
-    add("G", lambda: g.iota(T.iot[:, :], [[1, RS]], 0, 0, allow_small_or_imprecise_dtypes=True), [], [R("iot")], 600.0)
-    add("V", lambda: g.vector.memset(T.wa[:, :], 0.0), [], [R("wa")], vd(1792))
+    qx = NP // XQ
+    loads = [("nui", T.nui[:, :], T.nu[:, :], R("nui")), ("msg", T.msg[:, :, 0:64], T.x[:, 0:NI], R("msg", 0, 64)),
+             ("nxi", T.nxi[:, :], T.nx[:, :], R("nxi"))]
+    loads += [("x", T.pool[:, qx * u:qx * u + qx], T.x[:, qx * u:qx * u + qx], R("pool", qx * u, qx * u + qx)) for u in range(XQ)]
+    loads.insert(5, ("voli", T.voli[:, :], T.vol[:, :], R("voli")))
+    loads += [("lei", T.lei[:, :], T.le[:, :], R("lei")), ("x", T.pool[:, NP:NW], T.x[:, NP:NW], R("pool", NP, NW)),
+              ("lagi", T.lagi[:, :], T.lag[:, :], R("lagi"))]
+    for u, (_, out, in_, wr) in enumerate(loads):
+        dma("Y", out, in_, [], [wr], DMA + 400 * u)
+    add("G", lambda: g.iota(T.pci[:, :], [[0, 1]], 0, 1), [], [R("pci")], 130.0)
+    iota(full("iot"), [[1, RS]])
+    iota(R("pat", 0, 128), [[1, 8], [0, 16]])
+    iota(full("ohw"), [[32, NC], [0, 2]])
+    fill(R("st", 0, MID))
+    cp("S", R("st", MID, NW + NI), R("st", 0, NW + NI - MID))
+
+    def selector(z, w):
+        scaled(R(z, 0, 144), R("z1", 0, 144), w)
+
+    ts(col("pmi"), col("pci"), 15, A.bitwise_and)
+    cp("V", pc, col("pci"))
+    cp("V", pm, col("pmi"))
+    fill(half, 0.5)
+    ts(gc15, pc, pm, A.subtract, 15.0, A.add)
     cp("V", col("nuf"), col("nui"))
+    ts(R("oh", 0, 16), R("iot", 0, 16), pm, A.is_equal)
     add("V", lambda: g.vector.tensor_scalar(T.msg[:, :, 64], T.iot[:, 0:4], 0.0, T.nuf[:, 0:1], A.mult, A.add),
-        [R("iot"), R("nuf")], [R("msg", 64, 72)], vd(4))
+        [R("iot"), R("nuf")], [R("msg", 64, 72)], 64 * CY)
     send(5, [T.msg[:, s, 0:65] for s in range(4)], [T.rcv[:, s, 0:65] for s in range(4)], down, [R("msg")], [R("rcv")])
-    send(0, [T.pool[:, 3072 + 64 * s:3136 + 64 * s] for s in range(4)], [T.pool[:, NW + 64 * s:NW + 64 * s + 64] for s in range(4)],
-         up, [R("pool", 3072, NW)], [R("pool", NW, NW + NI)])
-    add("G", lambda: g.iota(T.ka[:, :], [[1, 16], [0, 16]], 0, 0, allow_small_or_imprecise_dtypes=True), [], [R("ka")], 600.0)
-    add("G", lambda: g.iota(T.kb[:, :], [[0, 16], [1, 16]], 0, 0, allow_small_or_imprecise_dtypes=True), [], [R("kb")], 600.0)
-    add("G", lambda: g.iota(T.iob[:, :], [[0, 4], [16, 16]], 0, 0, allow_small_or_imprecise_dtypes=True), [], [R("iob")], 300.0)
-    ts(col("pmi"), col("pci"), 15, None, A.bitwise_and)
-    cp("V", col("pm"), col("pmi"))
-    cp("V", col("pc"), col("pci"))
-    ts(col("gc15"), col("pc"), col("pm"), 15.0, A.subtract, A.add)
-    ts(R("zw", 0, 144), R("iot", 0, 144), col("gc15"), col("nuf"), A.is_equal, A.mult)
-    ts(R("oh", 0, 16), R("iot", 0, 16), col("pm"), None, A.is_equal)
-    ts(col("wnx"), col("oh", 0), col("oh", 1), None, A.add)
-    ts(col("wmu"), col("oh", 3), col("oh", 4), None, A.add)
-    ts(col("wo"), col("oh", 5), 16.0, col("oh", 6), A.mult, A.add)
-    ts(col("wn4"), col("oh", 4), -1.0, None, A.mult)
-    for z, w in (("zmu", col("wmu")), ("z1", 1.0), ("zn4", col("wn4")), ("znx", col("wnx")), ("zvol", col("oh", 2)),
-                 ("zo", col("wo")), ("z5", col("oh", 5)), ("z6", col("oh", 6))):
-        ts(R(z, 0, 144), R("iot", 0, 144), col("gc15"), w, A.is_equal, A.mult)
-    tt(R("m34", 0, 128), R("z1", 12, 140), R("z1", 11, 139), A.add)
-    ts(R("we", 512, 640), R("m34", 0, 128), col("nuf"), None, A.mult)
-    for s in range(4):
-        add("V", (lambda s=s: g.vector.tensor_scalar(T.we[:, 128 * s:128 * s + 128], T.m34[:, :], T.rcv[:, s, 64:65], None, A.mult)),
-            [R("m34"), R("rcv")], [R("we", 128 * s, 128 * s + 128)], vd(64))
-    ts(R("i256", 0, 128), R("iot", 0, 128), col("pc"), 256.0, A.is_equal, A.mult)
-    ts(R("base", 0, 64), R("iob", 0, 64), col("pm"), 1.0 / 256, A.add, A.mult)
-    ts(R("bi0", 0, 18), R("iot", 0, 18), -8.0, col("oh", 5), A.add, A.mult)
-    ts(R("bi", 0, 18), R("bi0", 0, 18), 16.0, None, A.mult)
-    ts(R("pmu", 0, 12), R("iot", 0, 12), 0.0, col("pm"), A.mult, A.add)
-    cp("V", R("lagr", 0, 16), R("lagi", 0, 16))
-    ts(R("ohw", 0, RS), R("iot", 0, RS), -128.0, None, A.add)
-    ts(R("olw", 0, RS), R("iot", 0, RS), 0.0, col("pm"), A.mult, A.add)
-    torow("wa", 5, "ohw")
-    torow("wa", 6, "olw")
-    add("G", lambda: g.iota(T.wb[:, :], [[0, NW + NI]], 0, 0, allow_small_or_imprecise_dtypes=True), [], [R("wb")], 7600.0,
-        after=sends[-1])
-    add("V", lambda: g.vector.memset(T.tt[:, 0:16], 0.0), [], [R("tt", 0, 16)], vd(16))
-    add("V", lambda: g.vector.memset(T.ss[:, :], 0.0), [], [R("ss")], vd(96))
-    add("V", lambda: g.vector.memset(T.volw[:, 192:RS], 0.0), [], [R("volw", 192, RS)], vd(16))
-    cp("V", R("volw", 0, 192), R("voli", 0, 192))
-    torow("wa", 2, "volw")
-    for c in ("c0", "c1", "c2"):
-        add("V", (lambda c=c: g.vector.memset(T[c][:, 192:RS], 0.0)), [], [R(c, 192, RS)], vd(16))
-    ts(col("wc3"), col("oh", 2), col("oh", 7), col("oh", 8), A.add, A.add)
-    ts(R("zc", 0, 144), R("iot", 0, 144), col("gc15"), col("wc3"), A.is_equal, A.mult)
-    ts(R("wi", 192, RS), R("olw", 0, 16), float(RS), None, A.mult)
-    cp("V", R("wc", 192, RS), R("iot", 192, RS))
-    ts(R("nii", 0, 192), R("nxi", 0, 192), 15, None, A.bitwise_and)
-    ts(R("nci", 0, 192), R("nxi", 0, 192), 4, None, A.arith_shift_right)
-    ts(R("p0", 0, 192), R("nii", 0, 192), float(RS), None, A.mult)
-    tt(R("lab", 0, 192), R("p0", 0, 192), R("nci", 0, 192), A.add)
-    ts(R("p1", 0, 192), R("nxi", 0, 192), -3071.5, 8192.0, A.add, A.mult)
-    ts(R("t2", 0, 192), R("nxi", 0, 192), 256.0, None, A.add)
-    tt(R("p1", 192, 384), R("p1", 0, 192), R("t2", 0, 192), A.min)
-    tt(R("t1", 0, 192), R("p1", 192, 384), R("lab", 0, 192), A.max)
-    cp("V", R("nxe", 0, 192), R("t1", 0, 192))
-    tt(R("dl", 0, 96), R("lab", 96, 192), R("lab", 0, 96), A.subtract)
-    tt(R("dab", 0, 192), R("lei", 0, 192), R("lei", 192, 384), A.subtract)
-    tt(R("dd", 0, 96), R("dab", 96, 192), R("dab", 0, 96), A.subtract)
+    iota(full("olw"), [[0, NC], [16, 2]])
+    iota(R("ka", 0, NI), [[32, 8], [0, 32]])
+    iota(R("kb", 0, NI), [[0, 8], [1, 32]])
+    ts(R("zw", 0, 144), R("iot", 0, 144), gc15, A.is_equal, col("nuf"), A.mult)
+    ts(R("z1", 0, 144), R("iot", 0, 144), gc15, A.is_equal)
+    ts(full("nii"), full("nxi"), 15, A.bitwise_and)
+    ts(full("nci"), full("nxi"), 4, A.arith_shift_right)
+    ts(full("p1"), full("nxi"), 0.5 - NP, A.add, 8192.0, A.mult)
+    ts(full("p0"), full("nii"), float(RS), A.mult)
+    tt(full("t2"), full("p1"), full("nxi"), A.min)
+    tt(R("p0", RS, 2 * RS), full("p0"), full("nci"), A.add)
+    ts(full("t1"), full("nxi"), float(NP), A.is_ge, float(NI), A.mult)
+    tt(full("p2"), R("p0", RS, 2 * RS), full("t2"), A.max)
+    cp("V", full("volw"), full("voli"))
+    torow("st", IH, full("ohw"))
+    torow("st", VO, full("volw"))
+    ts(full("p3"), full("p2"), ROUND16, A.add, -ROUND16, A.add)
+    cp("S", full("lab"), full("p2"))
+    tt(R("m34", 0, 128), R("z1", 15 - CH, 143 - CH), R("z1", 15 - CL, 143 - CL), A.add)
+    cp("S", full("hi"), full("p3"))
+    tt(full("lo"), full("p3"), full("lab"), A.subtract)
+    tt(full("hx"), full("p3"), full("t1"), A.add)
+    shifted(full("olw"), full("olw"), pm)
+    torow("st", IL, full("olw"))
+    ts(wt(2), oh(HI), oh(IH), A.add)
+    ts(wt(3), oh(IL), oh(LO), A.subtract)
+    ts(sq("dg", 0), R("iot", 0, 128), pc, A.is_equal)
     h = RS // XQ
     for u in range(XQ):
-        unwrap("p5", h * u, "zw", R("pool", 16 * h * u, 16 * h * (u + 1)),
-               (lambda j, u=u: T.pool[:, 16 * h * u + j:16 * h * (u + 1):16]), h)
-    cp("S", R("mh", 0, RS), R("p5", 0, RS))
-    tt(R("ml", 0, RS), R("p5", 0, RS), R("mh", 0, RS), A.subtract)
-    torow("wa", 3, "mh")
-    torow("wa", 4, "ml")
+        unwrap16(R("p5", h * u, h * u + h), "zw", R("pool", qx * u, qx * u + qx))
+    cp("S", full("mh"), full("p5"))
+    torow("st", CH, full("mh"), "S")
+    tt(full("t2"), full("p2"), full("t1"), A.add)
+    tt(full("ml"), full("p5"), full("mh"), A.subtract)
+    torow("st", CL, full("ml"))
+    for row, src in ((HI, "hi"), (LO, "lo"), (HX, "hx"), (VO, "volw")):
+        torow("kw", row, full(src))
+    for k in (1, 2):
+        scaled(sq("dg", k), sq("dg", 0), wt(k + 1))
+    scaled(sq("we", 4), R("m34", 0, 128), col("nuf"))
+    ts(R("bi", 0, 18), R("iot", 0, 18), -float(NI), A.mult, wt(2), A.mult)
+    ts(wt(5), oh(CH), oh(CL), A.add)
+    ts(wt(4), oh(DH), oh(DL), A.add, oh(LO), A.subtract)
+    ts(wt(7), oh(P0), oh(P1), A.add, oh(P2), A.add)
+    ts(gi, gc15, -15.0, A.add, 1.0 / 16, A.mult)
+    ts(wt(6), wt(4), oh(HI), A.add)
+    cp("V", R("nxe", RS, 2 * RS), full("t2"))
+    ts(R("pat", 0, 128), R("pat", 0, 128), gi, A.is_equal)
+    ts(wt(1), oh(G0), oh(G1), A.add, oh(G2), A.add)
+    ts(wt(9), pm, PL - 1.5, A.is_lt, 128.0, A.mult)
+    ts(wt(10), oh(IH), oh(IL), A.add)
+    ts(wt(8), wt(1), -1.0, A.mult)
+    rows("p7", [], [], None, R("st", NP, NW), 12)
+    dma("Y", T.kw[:, NP:NW], T.st[:, NP:NW], [R("st", NP, NW)], [R("kw", NP, NW)])
+    rows("p6", [(0, NI, ap(sq("we", 4)), T.pool[:, 0:NI])], [R("pool", 0, NI), sq("we", 4)], "tba", blk("vw", 1), 0)
+    ts(wt(0), oh(HX), oh(LO), A.subtract)
+    tt(R("dl", 0, 16), R("lab", NC, NC + 16), R("lab", 0, 16), A.subtract)
+    ts(R("base", 0, 16), R("iot", 0, 16), 16.0, A.mult, pm, A.add)
+    ts(R("base", 16, 32), R("base", 0, 16), 1.0 / NI, A.mult)
+    ts(R("fb", 0, 16), R("iot", 0, 16), 16.0, A.mult)
+    ts(R("fb", 16, 32), R("iot", 0, 16), 16.0, A.mult, 128.0 * (PL - 1), A.add)
+    ts(R("fb", 32, 48), R("iot", 0, 16), 0.0, A.mult, pm, A.add)
+    ts(pr, pm, float(RS), A.mult)
+    ts(R("qq", 0, 16), R("iot", 0, 16), pr, A.add)
+    for s in range(4):
+        add("V", (lambda s=s: g.vector.tensor_scalar(ap(sq("we", s)), T.m34[:, :], T.rcv[:, s, 64:65], None, A.mult)),
+            [R("m34"), R("rcv")], [sq("we", s)], 64 * CY)
+    selector("zmu", wt(5))
+    selector("zvol", oh(VO))
+    rows("p7", [(64 * s, 64 * s + 64, ap(sq("we", s)), T.rcv[:, s, 0:64]) for s in range(4)], [R("rcv"), R("we", 0, 512)], "tbe",
+         R("st", NW, NW + NI), None)
+    scaled(sq("bw", 0), R("pat", 0, 128), wt(7))
+    scaled(sq("bw", 1), R("pat", 0, 128), wt(8))
+    send(0, [T.pool[:, NP + 64 * s:NP + 64 * s + 64] for s in range(4)], [T.pool[:, NW + 64 * s:NW + 64 * s + 64] for s in range(4)],
+         up, [R("pool", NP, NW), R("st", 0, NP, [CL])], [R("pool", NW, NW + NI)])
+    for k in range(1, PL):
+        select(sq("zd", k), sq("bw", 0), [[0, 8], [-1, 16]], k - 1)
+    select(R("zc", 0, 128), R("pat", 0, 128), [[-16, 8], [-3, 16]], -3, 1)
+    tt(full("dab"), full("lei"), R("lei", RS, 2 * RS), A.subtract)
+    cp("V", R("lagr", 0, 16), R("lagi", 0, 16))
+    cp("V", R("ohw", 0, 16), R("lagi", 0, 16))
+    tt(ha("d4"), hb("hi"), ha("hi"), A.subtract)
+    tt(R("lagr", 16, 32), R("lagr", 0, 16), R("ohw", 0, 16), A.subtract)
+    tt(ha("d4", RS), ha("lo"), hb("lo"), A.subtract)
+    cp("V", R("volw", 0, 16), R("lagr", 16, 32))
+    ts(hb("d4"), ha("d4"), -1.0, A.mult)
+    ts(hb("d4", RS), ha("d4", RS), -1.0, A.mult)
+    tt(ha("dd"), hb("dab"), ha("dab"), A.subtract)
+    tt(R("olw", 0, 16), R("lagr", 16, 32), R("volw", 0, 16), A.subtract)
+    for row, src in ((G0, "ohw"), (G1, "volw"), (G2, "olw")):
+        torow("kw", row, full(src))
+    ts(wt(11), pc, 16.0, A.add)
+    ts(wt(12), pm, 2.5, A.is_lt)
+    ts(R("dp", 0, 160), R("iot", 0, 160), wt(11), A.is_equal, wt(7), A.mult)
+    ts(R("dp", 160, 320), R("iot", 0, 160), wt(11), A.is_equal, wt(8), A.mult)
+    scaled(sq("bw", 2), R("pat", 0, 128), wt(12))
+    selector("zn", wt(6))
+    selector("zf", wt(9))
+    selector("zo", wt(10))
+    selector("zx", wt(0))
+    tt(sq("zd", 1), sq("zd", 1), sq("bw", 1), A.add)
+    tt(R("zc", 0, 128), R("zc", 0, 128), sq("bw", 2), A.add)
 
-    def rows(blocks, rd, tb, dst, bias):
-        mm([(T.p6[:, lo:hi], l, r, hi - lo, True, True) for lo, hi, l, r in blocks], rd + [R("we")], [R("p6", 0, NI)])
-        cp("S", R(tb, 0, NI), R("p6", 0, NI))
-        it = [(T.p7[:, 0:NI], T.zn4[:, 11:139], T[tb][:, :], NI, True, False)]
-        if bias is not None:
-            it.append((T.p7[:, 0:NI], T.z5[:, 10:138], T.ka[:, :], NI, False, False))
-            it.append((T.p7[:, 0:NI], T.z6[:, 9:137], T.kb[:, :], NI, False, False))
-        for b, (lo, hi, l, r) in enumerate(blocks):
-            it.append((T.p7[:, lo:hi], l, r, hi - lo, False, b == len(blocks) - 1))
-        mm(it, rd + [R("we"), R(tb), R("zn4"), R("z5"), R("z6"), R("ka"), R("kb")], [R("p7", 0, NI)])
-        if bias is None:
-            cp("S", dst, R("p7", 0, NI))
+    Q = lambda k, lo=0, hi=16: R("qq", 32 * k + lo, 32 * k + hi)
+    F = lambda k: R("qq", 32 * k + 48, 32 * k + 64)
+    OF = R("qq", 32 * (PL + 2), 32 * (PL + 2) + 16)
+    entry = lambda i: blk("vw", i) if i > 1 else blk("b0", 0)
+    dbank = lambda k: ("p4", "p5", "p7")[k % 3]
+
+    def walk(k):
+        if k <= SHARE:
+            gather("V", R("vw", NI * k, NI * k + 128), R("kw", 0, NW), Q(k - 1, 0, 8))
+            gather("S", R("vw", NI * k + 128, NI * k + NI), R("kw", 0, NW), Q(k - 1, 8, 16))
         else:
-            add("S", lambda: g.scalar.activation(ap(dst), T.p7[:, 0:NI], IDENT, bias=T.bi[:, bias:bias + 1]),
-                [R("p7", 0, NI), R("bi")], [dst], vd(NI))
+            gather("S", blk("vw", k), R("kw", 0, NW), Q(k - 1))
 
-    def weights(s):
-        return T.we[:, 128 * s:128 * s + 128]
+    def move(k):
+        gather("S", blk("vg", k - 1), R("vw", 0, NI * (k + 1)), F(k))
 
-    rows([(64 * s, 64 * s + 64, weights(s), T.rcv[:, s, 0:64]) for s in range(4)], [R("rcv")], "tbe", R("wa", NW, NW + NI), None)
-    rows([(0, NI, weights(4), T.pool[:, 0:NI])], [R("pool", 0, NI)], "tba", R("vw", NI, 2 * NI), 0)
+    def scatter(k):
+        add("V", lambda: g.vector.tensor_copy(T.st[:, 0:NW].indirect(ap(Q(k))), ap(blk("vg", k - 1))),
+            [blk("vg", k - 1), Q(k)], [R("st", 0, NW)], 50 + NI * SC * CY)
 
+    done = {}
+
+    def dsum(k, upto, most=PL):
+        if k > KEEP + 1:
+            terms = [(0, R("zc", 0, 128), blk("ck", 0))] + [(i, sq("zd", i), entry(i)) for i in range(KEEP + 1, k + 1)]
+        else:
+            terms = [(i, sq("zd", i), entry(i)) for i in range(1, k + 1)]
+        lo = done.get(k, 0)
+        idx = [i for i in range(lo, len(terms)) if terms[i][0] <= upto][:most]
+        done[k] = lo + len(idx)
+        if idx:
+            mm([(T[dbank(k)][:, 0:NI], ap(terms[i][1]), ap(terms[i][2]), i == 0, i == len(terms) - 1) for i in idx],
+               [r for i in idx for r in terms[i][1:]], [R(dbank(k), 0, NI)])
+        return len(idx)
+
+    def sign(k):
+        o = R(dbank(k), 0, NI)
+        if k <= VSIGN:
+            ts(blk("sg", k - 1), o, 0.0, A.is_ge, 2.0, A.mult)
+        else:
+            shifted(blk("sg", k - 1), o, half, SIGN)
+
+    def keep(i):
+        it = [T.dp[:, 176 + G0:304 + G0]] if i == 1 else []
+        it += [T.dp[:, 16 + P0 - 3 * i:144 + P0 - 3 * i]]
+        mm([(T.p6[:, 0:NI], l, ap(entry(i)), i == 1 and x == 0, i == KEEP) for x, l in enumerate(it)], [R("dp"), entry(i)], [R("p6", 0, NI)])
+
+    def kept(k):
+        if k == KEEP:
+            cp("S", blk("ck", 0), R("p6", 0, NI))
+
+    fbank = lambda k: R("p%d" % (2 + k % 2), 0, 16) if k in APART else R("p%d" % ((k + 1) % 2), 16, 32)
+
+    def foot(k):
+        unwrap16(fbank(k), "zf", blk("sg", k - 1), [R("fb", 0, 16) if k <= VSIGN else R("fb", 16, 32), R("fb", 32, 48)])
+
+    fixed[0] = True
     for t in range(NR):
-        wc, wn = ("wa", "wb") if t % 2 == 0 else ("wb", "wa")
-        phase[0] = ""
-        seen.clear()
-        for row in (3, 4, 5, 6):
-            if t == NR - 1 and row < 5:
-                continue
-            dma("Y", T[wn][row:128:16, 0:NW], T[wc][row:128:16, 0:NW], [R(wc, 0, NW, row)], [R(wn, 0, NW, row)], 53248)
-        for e, lo, hi in XCH:
-            gather(e, R("gx", 16 * lo, 16 * hi), R(wc, 0, NW + NI), R("nxe", lo, hi))
-        if t > 0:
-            unwrap("p0", 0, "zo", R(wc, 0, NW), (lambda j, wc=wc: T[wc][:, RS * j + 192:RS * j + RS]), 16)
-            ts(R("ofo", 0, 16), R("p0", 0, 16), 2048.0, None, A.add)
-        for lo, hi in XPE:
-            unwrap("p5", lo, "zmu", R("gx", 16 * lo, 16 * hi), (lambda j, lo=lo, hi=hi: T.gx[:, 16 * lo + j:16 * hi:16]), hi - lo)
+        last = t == NR - 1
+        alo, so = NW + NI * t, NI * (t - 1)
+        sold, sn = R("p5", 384 - NC * (t % 2), 480 - NC * (t % 2)), R("p5", 288 + NC * (t % 2), 384 + NC * (t % 2))
+        dma("Y", T.kw[3:128:4, 0:NP], T.st[3:128:4, 0:NP], [R("st", 0, NP, range(3, 16, 4))], [R("kw", 0, NP, range(3, 16, 4))])
         if t == 0:
-            for lo, hi in XPE:
-                unwrap("p4", lo, "zvol", R("gx", 16 * lo, 16 * hi), (lambda j, lo=lo, hi=hi: T.gx[:, 16 * lo + j:16 * hi:16]), hi - lo)
-            cp("S", R("voln", 0, 192), R("p4", 0, 192))
-        tt(R("pp", 0, 96), R("p5", 0, 96), R("dab" if t == 0 else "ab", 0, 96), A.mult)
-        tt(R("p5", 384, 480), R("p5", 96, 192), R("dab" if t == 0 else "ab", 96, 192), A.mult)
-        tt(R("cn", 0, 192), R("p5", 0, 192), R("voln", 0, 192), A.mult)
-        tt(R("p5", 192, 288), R("p5", 384, 480), R("pp", 0, 96), A.subtract)
-        tt(R("p5", 288, 384), R("p5", 192, 288), R("ss", 0, 96), A.is_lt)
-        sn = R("p5", 288, 384)
-        tt(R("p5", 192, 288), sn, R("dl", 0, 96), A.mult)
-        tt(R("p1", 0, 96), R("p5", 192, 288), R("lab", 0, 96), A.add)
-        tt(R("p1", 96, 192), R("lab", 96, 192), R("p5", 192, 288), A.subtract)
-        cp(SPLIT, R("wi", 0, 192), R("p1", 0, 192))
-        tt(R("wc", 0, 192), R("p1", 0, 192), R("wi", 0, 192), A.subtract)
-        cp("V", R("qq", 32, 48), R("p1", 0, 16))
-        torow(wc, 0, "wi")
-        torow(wc, 1, "wc")
-        tt(R("dcn", 0, 96), R("cn", 96, 192), R("cn", 0, 96), A.subtract)
-        tt(R("p5", 384, 480), sn, R("dcn", 0, 96), A.mult)
-        tt(R("p2", 0, 96), R("p5", 384, 480), R("cn", 0, 96), A.add)
-        tt(R("p2", 96, 192), R("cn", 96, 192), R("p5", 384, 480), A.subtract)
-        cp(SPLIT, R("c0", 0, 192), R("p2", 0, 192))
-        tt(R("p3", 0, 192), R("p2", 0, 192), R("c0", 0, 192), A.subtract)
-        cp(SPLIT, R("c1", 0, 192), R("p3", 0, 192))
-        tt(R("c2", 0, 192), R("p3", 0, 192), R("c1", 0, 192), A.subtract)
-        torow(wc, 2, "c0")
-        torow(wc, 7, "c1", "S")
-        torow(wc, 8, "c2")
-        if t < NR - 1:
-            cp("V", R("ss", 0, 96), sn)
-            tt(R("ee", 0, 96), sn, R("dd", 0, 96), A.mult)
-            tt(R("ab", 0, 96), R("dab", 0, 96), R("ee", 0, 96), A.add)
-            tt(R("ab", 96, 192), R("dab", 96, 192), R("ee", 0, 96), A.subtract)
+            for x, (e, lo, hi) in enumerate(XCH0):
+                gather(e, R("gx", 16 * lo, 16 * hi), R("st", 0, NW + NI), R("nxe", RS + lo, RS + hi))
+                if x % 2:
+                    for bank, z in (("p5", "zmu"), ("p4", "zvol")):
+                        unwrap16(R(bank, hi - 64, hi), z, R("gx", 16 * hi - 1024, 16 * hi))
+            cp("S", full("voln"), full("p4"))
         else:
-            tt(R("dn", 0, 96), R("nxi", 96, 192), R("nxi", 0, 96), A.subtract)
-            tt(R("ee", 0, 96), sn, R("dn", 0, 96), A.mult)
-            tt(R("ynb", 0, 96), R("nxi", 0, 96), R("ee", 0, 96), A.add)
-            tt(R("ynb", 96, 192), R("nxi", 96, 192), R("ee", 0, 96), A.subtract)
-            dma("Y", T.yn[:, :], T.ynb[:, :], [R("ynb")], [], 98304)
-        alo = NW + NI * t
+            unwrap16(R("p0", 0, 16), "zo", R("st", NP, NW))
+            for x, (e, lo, hi) in enumerate(XCH):
+                gather(e, R("gx", 16 * lo, 16 * hi), R("st", 0, NW + NI), R("nxe", lo, hi))
+                if x == 0:
+                    cp("V", OF, R("p0", 0, 16))
+                if x == 1:
+                    gather("S", R("snd", so, so + NI), R("pool", 0, alo), OF)
+                    send(t, [T.snd[:, so + 64 * s:so + 64 * s + 64] for s in range(4)],
+                         [T.pool[:, alo + 64 * s:alo + 64 * s + 64] for s in range(4)], up, [R("snd", so, so + NI)], [R("pool", alo, alo + NI)])
+                j0, j1 = lo // 12, hi // 12
+                if j0 < j1:
+                    unwrap(full("p5"), "zmu", R("gx", RS * j0, RS * j1), lambda j: T.gx[:, RS * j:RS * j + RS], j0, j1)
+            cp("S", blk("vw", 1), blk("vw", 0))
+        co = "dab" if t == 0 else "ab"
+        tt(ha("xa"), ha("p5"), ha(co), A.mult)
+        tt(ha("p5", RS), hb("p5"), hb(co), A.mult)
+        tt(ha("cn"), ha("p5"), ha("voln"), A.mult)
+        tt(ha("p1"), hb("p5"), hb("voln"), A.mult)
+        tt(ha("df"), ha("p5", RS), ha("xa"), A.subtract)
+        tt(ha("dcn"), ha("p1"), ha("cn"), A.subtract)
         if t > 0:
-            so = NI * (t - 1)
-            gather("S", R("snd", so, so + NI), R("pool", 0, alo), R("ofo", 0, 16))
-            send(t, [T.snd[:, so + 64 * s:so + 64 * s + 64] for s in range(4)],
-                 [T.pool[:, alo + 64 * s:alo + 64 * s + 64] for s in range(4)], up, [R("snd", so, so + NI)], [R("pool", alo, alo + NI)])
-            cp("S", R("vw", NI, 2 * NI), R("vw", 0, NI))
-            sb, sr = "snd", so
+            tt(sn, ha("df"), sold, A.is_lt)
         else:
-            sb, sr = "pool", 3072
-        if t < NR - 1:
-            rows([(64 * s, 64 * s + 64, weights(s), T[sb][:, sr + 64 * s:sr + 64 * s + 64]) for s in range(4)],
-                 [R(sb, sr, sr + NI)], "tbe", R(wn, NW, NW + NI), None)
-        rows([(0, NI, weights(4), T.pool[:, alo:alo + NI])], [R("pool", alo, alo + NI)], "tba", R("vw", 0, NI), 13 + t)
-        if t == NR - 1:
-            dma("Y", T.y[:, 0:NI], T.pool[:, alo:alo + NI], [R("pool", alo, alo + NI)], [], 65536)
-        co = 0
-        first = len(ops)
-        for k in range(1, PL):
-            lo, s0, s1 = NI * k, 16 * k, 16 * k + 16
+            ts(sn, ha("df"), 0.0, A.is_lt)
+        tt(ha("ee"), sn, ha("dcn"), A.mult)
+        for x, row in enumerate((DH, DL)):
+            tt(ha("dy", RS * x), sn, ha("d4", RS * x), A.mult)
+            tt(hb("dy", RS * x), sn, hb("d4", RS * x), A.mult)
+            torow("kw", row, R("dy", RS * x, RS * x + RS))
+        tt(hb("pp"), ha("p1"), ha("ee"), A.subtract)
+        tt(ha("pp"), ha("ee"), ha("cn"), A.add)
+        tt(R("q1", 0, 16), R("p5", sn[2], sn[2] + 16), R("dl", 0, 16), A.mult)
+        cp("S", full("c0"), full("pp"))
+        torow("kw", P0, full("c0"), "S")
+        ts(full("p1"), full("pp"), ROUND128, A.add, -ROUND128, A.add)
+        tt(R("q1", 16, 32), R("q1", 0, 16), R("lab", 0, 16), A.add)
+        tt(R("q1", 32, 48), R("pp", 0, 16), R("lagr", 0, 16), A.is_ge)
+        tt(full("c2"), full("pp"), full("p1"), A.subtract)
+        torow("kw", P2, full("c2"))
+        tt(full("c1"), full("p1"), full("c0"), A.subtract)
+        torow("kw", P1, full("c1"))
+        cp("V", Q(1), R("q1", 16, 32))
+        tt(R("q1", 48, 64), R("q1", 32, 48), R("base", 16, 32), A.add)
+        if last:
+            tt(ha("dn"), hb("nxi"), ha("nxi"), A.subtract)
+        step, old, new = ("dn", "nxi", "ynb") if last else ("dd", "dab", "ab")
+        tt(ha("p5", RS), sn, ha(step), A.mult)
+        ts(F(1), R("q1", 48, 64), float(NI), A.mult)
+        rows("p6", [(0, NI, ap(sq("we", 4)), T.pool[:, alo:alo + NI])], [R("pool", alo, alo + NI), sq("we", 4)], "tba", blk("vw", 0), 13 + t)
+        tt(ha(new), ha("p5", RS), ha(old), A.add)
+        tt(hb(new), hb(old), ha("p5", RS), A.subtract)
+        if last:
+            dma("Y", T.yn[:, :], T.ynb[:, :], [R("ynb")], [])
+            dma("Y", T.y[:, 0:NI], T.pool[:, alo:alo + NI], [R("pool", alo, alo + NI)], [])
+        else:
+            sb, sr = ("snd", so) if t > 0 else ("pool", NP)
+            rows("p3", [(64 * s, 64 * s + 64, ap(sq("we", s)), T[sb][:, sr + 64 * s:sr + 64 * s + 64]) for s in range(4)],
+                 [R(sb, sr, sr + NI), R("we", 0, 512)], "tbe", R("st", NW, NW + NI), None)
+        move(1)
+        done.clear()
+        for k in range(2, PL):
+            bank = "p%d" % (k % 2)
+            wide = 16 if k == 2 or k - 1 in APART else 32
 
-            def at(name, k=k, first=first):
-                hint[0] = (first + 7, (k - 2) * PERIOD + PLAN[name]) if k > 1 else None
+            def ahead(k):
+                used = dsum(k + 1, k)
+                if KEEP < k < PL - 2:
+                    dsum(k + 2, k, max(0, AHEAD - used))
 
-            def move(k, wn=wn, at=at):
-                vo, qi = R("vg", NI * (k - 1), NI * k), R("qq", 32 * k, 32 * k + 16)
-                at("v", k)
-                gather("S", vo, R("vw", 0, NI * (k + 1)), R("qq", 32 * k + 80, 32 * k + 96))
-                at("s", k)
-                add("V", (lambda: g.vector.tensor_copy(T[wn][:, 0:NW].indirect(ap(qi)), ap(vo))),
-                    [vo, qi], [R(wn, 0, NW)], 50 + NI * SC * CY)
-            if k > 1:
-                at("g")
-                gather("S", R("vw", lo, lo + NI), R(wc, 0, NW), R("qq", 2 * s0 - 32, 2 * s0 - 16))
-                bank, cb = "p%d" % (k % 2), "p%d" % (2 + k % 2)
-                at("n" if k < PL - 1 else "c")
-                unwrap(bank, 0, "znx", R("vw", lo, lo + NI), (lambda j, lo=lo: T.vw[:, lo + j:lo + NI:16]), 16)
-                at("q")
-                w = 32 if k > 3 else 16
-                cp("V", R("qq", 2 * s0, 2 * s0 + w), R(bank, 0, w))
-                if k > 3:
-                    move(k - 2)
-                at("c" if k < PL - 1 else "n")
-                unwrap(cb, 0, "zc", R("vw", lo, lo + NI), (lambda j, lo=lo: T.vw[:, lo + j:lo + NI:16]), 16, PIECE)
-                at("u")
-                tt(R("uu", s0, s1), R(cb, 0, 16), R("uu", s0 - 16, s0), A.add)
-                at("t")
-                if k < PL - 1:
-                    tt(R("tt", s0, s1), R(cb, 0, 16), R("tt", s0 - 16, s0), A.add)
-            else:
-                tt(R("uu", 16, 32), R("p2", 0, 16), R("lagr", 0, 16), A.subtract)
-                cp("V", R("tt", 16, 32), R("p2", 0, 16))
-            at("m")
-            add("V", (lambda k=k, co=co: g.vector.tensor_tensor(
-                T.cmp[:, co:co + 16 * k], T.uu[:, 16 * k:16 * k + 16].indirect(T.pmu[:, 0:k]), T.tt[:, 0:16 * k], A.is_ge)),
-                [R("uu", s0, s1), R("pmu"), R("tt", 0, s0)], [R("cmp", co, co + s0)], 50 + s0 * GA * CY)
-            nb = "p%d" % (k % 2) if 1 < k < PL - 2 else ("p4" if k % 2 == 1 else "p7")
-            at("k")
-            mm([(T[nb][:, 16:32], T.i256[:, :], T.base[:, 0:16], 16, True, False)]
-               + [(T[nb][:, 16:32], T.i256[:, :], T.cmp[:, co + 16 * j:co + 16 * j + 16], 16, False, j == k - 1) for j in range(k)],
-               [R("i256"), R("base"), R("cmp", co, co + s0)], [R(nb, 16, 32)])
-            co += s0
-            if not 1 < k < PL - 2:
-                at("o")
-                cp("V", R("qq", 2 * s0 + 80, 2 * s0 + 96), R(nb, 16, 32))
-                move(k)
-            hint[0] = None
-    wf = "wb" if NR % 2 == 1 else "wa"
-    phase[0] = "z"
-    for bank, lo, hi in (("p5", 0, 64), ("p6", 64, 128), ("p0", 128, 192)):
-        unwrap(bank, 0, "zo", R(wf, 0, NW), (lambda j, lo=lo, hi=hi: T[wf][:, RS * j + 16 + lo:RS * j + 16 + hi]), hi - lo)
-        ts(R("ofy", lo, hi), R(bank, 0, hi - lo), 2048.0, None, A.add)
-    for e, lo, hi in YCH:
+            calls = {"g": walk, "b": lambda k: gather("S", blk("b0", 0), R("kw", 0, NW), Q(0)),
+                     "n": lambda k: unwrap16(R(bank, 0, 16), "zn", blk("vw", k)), "q": lambda k: cp("V", Q(k, 0, wide), R(bank, 0, wide)),
+                     "d": lambda e: dsum(e, k), "a": ahead, "k": keep, "c": kept, "s": sign, "f": foot,
+                     "o": lambda k: cp("V", F(k), fbank(k)), "m": move, "w": scatter}
+            for x in STEP.get(k, STEP[0]).split():
+                calls[x[0]](k - int(x[1:] or 0))
+            if t == 0 and 6 <= k < 10:
+                unwrap(full("p6"), "zx", R("kw", 0, NP), lambda j: T.kw[:, j:NP:16], 4 * k - 24, 4 * k - 20)
+            if t == 0 and k == 10:
+                cp("V", full("nxe"), full("p6"))
+    for bank, lo, hi in (("p5", 0, 64), ("p6", 64, 128), ("p7", 128, 176)):
+        unwrap(R(bank, 0, hi - lo), "zo", R("st", 0, NP), lambda j, lo=lo, hi=hi: T.st[:, RS * j + 16 + lo:RS * j + 16 + hi])
+    unwrap16(R("p7", 48, 64), "zo", R("st", NP, NW))
+    for x, (e, lo, hi) in enumerate(YCH):
+        if x % 2 == 0:
+            cp("V", R("ofy", lo, lo + 64), R(("p5", "p6", "p7")[x // 2], 0, 64))
         gather(e, R("gx", 16 * lo, 16 * hi), R("pool", 0, NW + NR * NI), R("ofy", lo, hi))
-        dma("Y", T.y[:, NI + 16 * lo:NI + 16 * hi], T.gx[:, 16 * lo:16 * hi], [R("gx", 16 * lo, 16 * hi)], [], 4096 * (hi - lo))
+        dma("Y", T.y[:, NI + 16 * lo:NI + 16 * hi], T.gx[:, 16 * lo:16 * hi], [R("gx", 16 * lo, 16 * hi)], [])
     return ops, q, nrl[0]
 
 
 def depend(ops):
-    n = len(ops)
-    dep = [dict() for _ in range(n)]
+    dep = [set() for _ in ops]
     hist = {}
     for i, o in enumerate(ops):
-        d = dep[i]
         for kind, regs in (("r", o["rd"]), ("w", o["wr"]), ("x", o["ex"])):
             for r in regs:
                 for j, k2, r2 in hist.get(r[0], []):
-                    if j == i or not overlap(r, r2):
-                        continue
-                    if kind == "r" and k2 == "w":
-                        d[j] = True
-                    elif kind == "w" and k2 != "x":
-                        d.setdefault(j, False)
-                    elif kind == "x" and k2 == "x" and (ops[j]["eng"] != o["eng"] or o["eng"] == "P"):
-                        d.setdefault(j, False)
+                    if overlap(r, r2) and ((kind == "r" and k2 == "w") or (kind == "w" and k2 != "x")
+                                           or (kind == "x" and k2 == "x" and (ops[j]["eng"] != o["eng"] or o["eng"] == "P"))):
+                        dep[i].add(j)
         for kind, regs in (("r", o["rd"]), ("w", o["wr"]), ("x", o["ex"])):
             for r in regs:
                 hist.setdefault(r[0], []).append((i, kind, r))
+        if o["kind"] == "a":
+            dep[i].add(i - 1)
     return dep
 
 
-def order(ops, dep, shift):
+def order(ops, dep):
     n = len(ops)
-    succ = [[] for _ in range(n)]
-    pre = [list(dep[i]) + ([ops[i]["after"]] if ops[i]["after"] is not None else []) for i in range(n)]
-    for i in range(n):
-        for j in pre[i]:
-            succ[j].append(i)
+    dep = [set(d) for d in dep]
+    tail, chain = {}, set()
+    for i, o in enumerate(ops):
+        if o["fixed"] and o["eng"] is not None:
+            if o["eng"] in tail and tail[o["eng"]] not in dep[i]:
+                dep[i].add(tail[o["eng"]])
+                chain.add((tail[o["eng"]], i))
+            tail[o["eng"]] = i
+    gap = lambda j, i: -ops[j]["lat"] if (j, i) in chain else 0.0 if ops[j]["eng"] == ops[i]["eng"] == "P" else WAKE
     prio = [0.0] * n
     for i in range(n - 1, -1, -1):
-        prio[i] = max(1.0, ops[i]["dur"] + ops[i]["lat"] + WAKE + shift.get(ops[i]["tag"], 0)) + max([prio[j] for j in succ[i]] + [0.0])
-    fin = [0.0] * n
-    start = [0.0] * n
+        prio[i] += ops[i]["dur"] + ops[i]["lat"]
+        for j in dep[i]:
+            prio[j] = max(prio[j], prio[i] + gap(j, i) + 0.01)
+    start, fin = [0.0] * n, [0.0] * n
     busy = {e: [] for e in ("V", "S", "P", "G", "Y")}
-    rank = sorted(range(n), key=lambda i: (-prio[i], i))
-    for i in rank:
-        t = 0.0
-        for j in pre[i]:
-            same = ops[j]["eng"] == ops[i]["eng"] and ops[j]["kind"] == "c"
-            if same and ops[i]["eng"] == "P":
-                t = max(t, start[j] + ops[j]["dur"])
-            else:
-                t = max(t, fin[j] + (WAKE0 if same else WAKE))
+    for i in sorted(range(n), key=lambda i: (-prio[i], i)):
+        t = max([fin[j] + gap(j, i) for j in dep[i]] + [0.0])
         e, d = ops[i]["eng"], ops[i]["dur"]
         if e is not None:
             l = busy[e]
@@ -448,15 +529,7 @@ def order(ops, dep, shift):
             l.insert(k, (t, t + d))
         start[i] = t
         fin[i] = t + d + ops[i]["lat"]
-    return start, fin, pre
-
-
-def sequence(ops, start, pre, move):
-    key = []
-    for i, o in enumerate(ops):
-        t = start[i] if o["hint"] is None else start[o["hint"][0]] + o["hint"][1]
-        key.append(max([t + move.get(o["tag"], 0)] + [key[j] + 0.001 for j in pre[i]]))
-    return sorted(range(len(ops)), key=lambda i: (key[i], i))
+    return sorted(range(n), key=lambda i: (start[i], i))
 
 
 def rank_program(g, core, T, topo):
@@ -464,43 +537,34 @@ def rank_program(g, core, T, topo):
         return
     ops, q, nrl = build(g, core, T, topo)
     dep = depend(ops)
-    start, fin, pre = order(ops, dep, SHIFT)
-    seq = sequence(ops, start, pre, MOVE)
+    seq = order(ops, dep)
     pos = {i: k for k, i in enumerate(seq)}
-    need = [[] for _ in ops]
-    for i, o in enumerate(ops):
-        if o["kind"] == "a":
-            continue
-        last = {}
-        for j, raw in dep[i].items():
-            p = ops[j]
-            if p["kind"] == "r":
-                continue
-            if p["kind"] == "c":
-                if p["eng"] == o["eng"] and o["kind"] == "c" and p["eng"] == "P":
-                    continue
-                if p["eng"] not in last or pos[j] > pos[last[p["eng"]]]:
-                    last[p["eng"]] = j
-            else:
-                need[i].append(j)
-        need[i] += list(last.values())
-    seen = {}
-    marked = set()
+    seen, marked = {}, set()
     waits = [[] for _ in ops]
     for i in seq:
-        e = ops[i]["eng"]
-        for j in need[i]:
-            key = (e, ops[j]["eng"]) if ops[j]["kind"] == "c" else (e, ops[j]["tok"][0])
+        o = ops[i]
+        if o["kind"] == "a":
+            continue
+        need = {}
+        for j in dep[i]:
+            p = ops[j]
+            if p["kind"] == "r" or (p["eng"] == "P" and o["eng"] == "P"):
+                continue
+            key = (o["eng"], p["eng"] if p["kind"] == "c" else p["tok"][0])
+            if key not in need or pos[j] > pos[need[key]]:
+                need[key] = j
+        for key, j in sorted(need.items(), key=lambda kj: pos[kj[1]]):
             if seen.get(key, -1) < pos[j]:
                 seen[key] = pos[j]
                 waits[i].append(j)
                 marked.add(j)
     count = {}
     for i in seq:
-        if ops[i]["kind"] == "c" and i in marked:
-            s = "c" + ops[i]["eng"]
+        o = ops[i]
+        if o["kind"] == "c" and i in marked:
+            s = "c" + o["eng"]
             count[s] = count.get(s, 0) + 1
-            ops[i]["tok"] = (s, count[s])
+            o["tok"] = (s, count[s])
     for i in seq:
         o = ops[i]
         if o["kind"] == "a":
@@ -513,5 +577,6 @@ def rank_program(g, core, T, topo):
         elif o["kind"] == "c" and i in marked:
             ins.then_inc(T.sem[o["tok"][0]], 1)
     g.wait_ge(T.sem.rl, nrl)
-    for i in sorted((i for i in seq if ops[i]["kind"] in "da" and i not in marked), key=lambda i: fin[i]):
-        g.wait_ge(T.sem[ops[i]["tok"][0]], ops[i]["tok"][1])
+    for i in seq:
+        if ops[i]["kind"] in "da" and i not in marked:
+            g.wait_ge(T.sem[ops[i]["tok"][0]], ops[i]["tok"][1])

from concourse.bass import DstId, RemoteDMATransfer
from concourse.mybir import AluOpType, ActivationFunctionType

NR, PL, NI, RS = 5, 12, 256, 192
NP, NW, NC = 16 * RS, 16 * RS + NI, RS // 2
DH, DL, VO, CH, P0, P1, P2, CL, G0, G1, G2, IH, HI, LO, HX, IL = range(16)
ROUND16, ROUND128 = 1.5 * 2.0 ** 27, 1.5 * 2.0 ** 30
XCH0 = [("V", 0, 34), ("S", 34, 64), ("V", 64, 98), ("S", 98, 128), ("V", 128, 162), ("S", 162, 192)]
XCH = [("V", 0, 24), ("S", 24, 60), ("V", 60, 108), ("S", 108, 144), ("V", 144, 168), ("S", 168, 180), ("V", 180, 192)]
YCH = [("S", 0, 34), ("V", 34, 64), ("S", 64, 98), ("V", 98, 128), ("S", 128, 162), ("V", 162, 192)]
XQ, MID = 4, 2048
SHARE, VSIGN = 4, 3
KEEP = 4
AHEAD = 4
APART = (2, 3, 11)
STEP = {2: "g b w1 n q d a k1 k", 3: "g s1 n d f1 k a q", 4: "g o2 m2 s1 n f1 d k a q o1 s w2",
        0: "g f1 n d q m2 c1 a s w2", PL - 1: "g f1 d n q m2 s w2 m1 f o m w1 w"}
NDMA = 100
CY, PCY, GA, SC, WAKE, DMA, REMOTE = 1.0, 0.5, 1.5, 3.5, 250.0, 1600.0, 3800.0

BF, F32, I32, U16 = "bfloat16", "float32", "int32", "uint16"
SCRATCH = {}
for _n, _w, _d in [
        ("pool", NW + NR * NI, BF), ("st", NW + NI, BF), ("kw", NW, BF), ("vw", PL * NI, BF), ("vg", 11 * NI, BF),
        ("gx", NP, BF), ("snd", 4 * NI, BF), ("tba", NI, BF), ("tbe", NI, BF), ("b0", 3 * NI, BF), ("ck", NI, BF), ("sg", 11 * NI, BF),
        ("nui", 1, I32), ("nxi", RS, I32), ("lei", 2 * RS, I32), ("voli", RS, I32), ("lagi", 16, I32),
        ("pci", 1, I32), ("pmi", 1, I32), ("nii", RS, I32), ("nci", RS, I32),
        ("iot", RS, F32), ("pc", 8, F32), ("nuf", 1, F32), ("oh", 16, F32), ("wt", 16, F32), ("bi", 18, F32),
        ("zw", 144, BF), ("z1", 144, BF), ("zmu", 144, BF), ("zvol", 144, BF), ("zo", 144, BF), ("zx", 144, BF), ("zn", 144, BF),
        ("zf", 144, BF), ("m34", 128, BF), ("we", 5 * 128, BF), ("dg", 3 * 128, BF), ("ka", NI, BF), ("kb", NI, BF),
        ("pat", 128, BF), ("bw", 3 * 128, BF), ("zd", PL * 128, BF), ("dp", 320, BF), ("zc", 128, BF), ("fb", 48, BF),
        ("lab", RS, F32), ("hi", RS, BF), ("lo", RS, BF), ("hx", RS, BF), ("d4", 2 * RS, BF), ("dy", 2 * RS, BF), ("dl", 16, F32),
        ("volw", RS, BF), ("ohw", RS, BF), ("olw", RS, BF), ("mh", RS, BF), ("ml", RS, BF),
        ("lagr", 32, F32), ("base", 32, F32), ("t1", RS, F32), ("t2", RS, F32), ("nxe", 2 * RS, U16),
        ("dab", RS, F32), ("dd", NC, F32), ("ab", RS, F32), ("xa", NC, F32), ("df", NC, F32), ("dn", NC, F32), ("ynb", RS, F32),
        ("q1", 64, F32), ("qq", 32 * (PL + 3), U16), ("ofy", RS, U16), ("pp", RS, F32), ("ee", NC, F32),
        ("voln", RS, F32), ("cn", NC, F32), ("dcn", NC, F32), ("c0", RS, BF), ("c1", RS, BF), ("c2", RS, BF)]:
    SCRATCH[_n] = ("sbuf", [128, _w], _d)
SCRATCH["msg"] = ("sbuf", [128, 4, 72], BF)
SCRATCH["rcv"] = ("sbuf", [128, 4, 72], BF)
for _b in range(8):
    SCRATCH["p%d" % _b] = ("psum", [128, 512], F32)
SEMAPHORES = ["cV", "cS", "cP", "cG", "rl"] + ["ar%d" % _k for _k in range(6)] + ["d%d" % _k for _k in range(NDMA)]

A = AluOpType
COPY, IDENT, SIGN = ActivationFunctionType.Copy, ActivationFunctionType.Identity, ActivationFunctionType.Sign


def overlap(a, b):
    return a[0] == b[0] and a[2] < b[3] and b[2] < a[3] and (a[1] is None or b[1] is None or bool(a[1] & b[1]))


def psum(r):
    return len(r[0]) == 2 and r[0][0] == "p" and r[0][1].isdigit()


def build(g, core, T, topo):
    rank = T.rank_of(core)
    n = len(T.cores)
    ops, fixed = [], [False]
    q = {"V": g.vector, "S": g.scalar, "P": g.tensor, "G": g, "Y": g.sync}

    def R(name, lo=0, hi=1 << 20, rows=None):
        return (name, None if rows is None else frozenset(rows), lo, hi)

    def col(name, k=0):
        return R(name, k, k + 1)

    def add(eng, fn, rd, wr, dur, kind="c", tok=None, lat=0.0):
        ops.append({"eng": eng, "fn": fn, "rd": rd, "wr": wr, "ex": [R(r[0]) for r in rd + wr if psum(r)], "kind": kind, "tok": tok,
                    "dur": dur, "lat": lat, "fixed": fixed[0]})

    def ap(r):
        return T[r[0]][:, r[2]:r[3]]

    def span(o, a=None, c=1.0):
        if a is not None and SCRATCH[o[0]][2] in (BF, U16) and SCRATCH[a[0]][2] in (BF, U16):
            c = 0.5
        return max(64.0, (o[3] - o[2]) * c) * CY

    def tt(o, a, b, op):
        add("V", lambda: g.vector.tensor_tensor(ap(o), ap(a), ap(b), op), [a, b], [o], span(o, None, 1 if psum(a) or psum(b) else 2))

    def ts(o, a, s1, op0, s2=None, op1=None):
        rd = [a] + [s for s in (s1, s2) if isinstance(s, tuple)]
        c1 = ap(s1) if isinstance(s1, tuple) else s1
        c2 = ap(s2) if isinstance(s2, tuple) else s2
        if op1 is None:
            add("V", lambda: g.vector.tensor_scalar(ap(o), ap(a), c1, None, op0), rd, [o], span(o, a))
        else:
            add("V", lambda: g.vector.tensor_scalar(ap(o), ap(a), c1, c2, op0, op1), rd, [o], span(o, a))

    def cp(eng, o, a):
        if eng == "V":
            add("V", lambda: g.vector.tensor_copy(ap(o), ap(a)), [a], [o], span(o, a))
        else:
            add("S", lambda: g.scalar.activation(ap(o), ap(a), COPY), [a], [o], span(o))

    def scaled(o, a, w):
        add("S", lambda: g.scalar.activation(ap(o), ap(a), COPY, scale=ap(w)), [a, w], [o], span(o))

    def shifted(o, a, b, func=IDENT):
        add("S", lambda: g.scalar.activation(ap(o), ap(a), func, bias=ap(b)), [a, b], [o], span(o))

    def fill(o, v=0.0):
        add("V", lambda: g.vector.memset(ap(o), v), [], [o], span(o, o))

    def iota(o, pattern):
        add("G", lambda: g.iota(ap(o), pattern, 0, 0, allow_small_or_imprecise_dtypes=True), [], [o], 130 + 2 * span(o))

    def select(o, a, pattern, base, by_row=0):
        add("G", lambda: g.affine_select(ap(o), ap(a), pattern, A.is_ge, 0.0, base, by_row), [a], [o], 170 + 2 * span(o))

    def gather(eng, o, win, off):
        d = 60 + (o[3] - o[2]) * GA * CY
        if eng == "V":
            add("V", lambda: g.vector.tensor_copy(ap(o), ap(win).indirect(ap(off))), [win, off], [o], d)
        else:
            add("S", lambda: g.scalar.activation(ap(o), ap(win).indirect(ap(off)), COPY), [win, off], [o], d)

    def mm(items, rd, wr):
        def fn():
            ins = None
            for o, l, r, st, sp in items:
                ins = g.tensor.matmul(o, l, r, st, sp)
            return ins
        add("P", fn, rd, wr, sum(it[0].shape[1] for it in items) * PCY)

    def unwrap(o, z, src, rhs, j0=0, j1=16, first=()):
        mm([(ap(o), ap(sq("dg", 0)), ap(f), x == 0, False) for x, f in enumerate(first)]
           + [(ap(o), T[z][:, 15 - j:143 - j], rhs(j), j == 0 and not first, j == 15) for j in range(j0, j1)],
           [R(z), src] + list(first) + ([sq("dg", 0)] if first else []), [o])

    def unwrap16(o, z, src, first=()):
        unwrap(o, z, src, lambda j: T[src[0]][:, src[2] + j:src[3]:16], 0, 16, first)

    def sq(name, k):
        return R(name, 128 * k, 128 * k + 128)

    nd = [0]

    def dma(eng, out, in_, rd, wr, lat=DMA):
        s = "d%d" % nd[0]
        nd[0] += 1
        add(eng, lambda: q[eng].dma_start(out, in_), rd, wr, 60.0, "d", (s, 16), lat)

    def torow(w, row, src, eng="Y"):
        dma(eng, T[w][row:128:16, 0:NP], ap(src), [src], [R(w, 0, NP, [row])])

    nrl = [0]

    def send(k, srcs, dsts, peers, rd, wr):
        trs = []
        for s in range(4):
            peer = T.cores[peers[s]]
            eng = topo.engines(core, peer)
            per = len(eng) // 4
            mask = sum(1 << e for e in eng[per * s:per * s + per])
            rid, pid, _ = topo.addr(peer)
            trs.append(RemoteDMATransfer(dst_ids=[DstId(rid=rid, pnc=pid)], dma_engine_mask=mask,
                                         remote_sem=T.sem["ar%d" % k], src=srcs[s], dst=dsts[s]))
            nrl[0] += per
        add("G", lambda: g.remote_dma_fused(trs, local_sem=T.sem.rl), rd, [], 500.0, "r")
        add(None, None, [], wr, 0.0, "a", ("ar%d" % k, 4 * per), REMOTE)

    up = [(rank + 1 + s) % n for s in range(4)]
    down = [(rank - 1 - s) % n for s in range(4)]
    full = lambda name: R(name, 0, RS)
    ha = lambda name, lo=0: R(name, lo, lo + NC)
    hb = lambda name, lo=0: R(name, lo + NC, lo + RS)
    blk = lambda name, k: R(name, NI * k, NI * k + NI)
    pc, pm, gc15, gi, half, pr = [col("pc", k) for k in range(6)]
    oh = lambda k: col("oh", k)
    wt = lambda k: col("wt", k)

    def rows(bank, blocks, rd, tb, dst, bias):
        o = R(bank, 0, NI)
        it = [] if bias is None else [(ap(o), ap(sq("dg", 1)), T.ka[:, :], True, False), (ap(o), ap(sq("dg", 2)), T.kb[:, :], False, not blocks)]
        if it:
            mm(it, [R("dg", 128, 384), R("ka"), R("kb")], [o])
        if blocks:
            mm([(T[bank][:, lo:hi], l, r, bias is None, True) for lo, hi, l, r in blocks], rd, [o])
        b = col("bi", bias or 0)
        if blocks:
            add("S", lambda: g.scalar.activation(T[tb][:, :], ap(o), IDENT, bias=ap(b), scale=ap(oh(CL))), [o, b, oh(CL)], [R(tb)], span(o))
            tt(dst, o, R(tb, 0, NI), A.subtract)
        else:
            ts(dst, o, b, A.subtract)

    qx = NP // XQ
    loads = [("nui", T.nui[:, :], T.nu[:, :], R("nui")), ("msg", T.msg[:, :, 0:64], T.x[:, 0:NI], R("msg", 0, 64)),
             ("nxi", T.nxi[:, :], T.nx[:, :], R("nxi"))]
    loads += [("x", T.pool[:, qx * u:qx * u + qx], T.x[:, qx * u:qx * u + qx], R("pool", qx * u, qx * u + qx)) for u in range(XQ)]
    loads.insert(5, ("voli", T.voli[:, :], T.vol[:, :], R("voli")))
    loads += [("lei", T.lei[:, :], T.le[:, :], R("lei")), ("x", T.pool[:, NP:NW], T.x[:, NP:NW], R("pool", NP, NW)),
              ("lagi", T.lagi[:, :], T.lag[:, :], R("lagi"))]
    for u, (_, out, in_, wr) in enumerate(loads):
        dma("Y", out, in_, [], [wr], DMA + 400 * u)
    add("G", lambda: g.iota(T.pci[:, :], [[0, 1]], 0, 1), [], [R("pci")], 130.0)
    iota(full("iot"), [[1, RS]])
    iota(R("pat", 0, 128), [[1, 8], [0, 16]])
    iota(full("ohw"), [[32, NC], [0, 2]])
    fill(R("st", 0, MID))
    cp("S", R("st", MID, NW + NI), R("st", 0, NW + NI - MID))

    def selector(z, w):
        scaled(R(z, 0, 144), R("z1", 0, 144), w)

    ts(col("pmi"), col("pci"), 15, A.bitwise_and)
    cp("V", pc, col("pci"))
    cp("V", pm, col("pmi"))
    fill(half, 0.5)
    ts(gc15, pc, pm, A.subtract, 15.0, A.add)
    cp("V", col("nuf"), col("nui"))
    ts(R("oh", 0, 16), R("iot", 0, 16), pm, A.is_equal)
    add("V", lambda: g.vector.tensor_scalar(T.msg[:, :, 64], T.iot[:, 0:4], 0.0, T.nuf[:, 0:1], A.mult, A.add),
        [R("iot"), R("nuf")], [R("msg", 64, 72)], 64 * CY)
    send(5, [T.msg[:, s, 0:65] for s in range(4)], [T.rcv[:, s, 0:65] for s in range(4)], down, [R("msg")], [R("rcv")])
    iota(full("olw"), [[0, NC], [16, 2]])
    iota(R("ka", 0, NI), [[32, 8], [0, 32]])
    iota(R("kb", 0, NI), [[0, 8], [1, 32]])
    ts(R("zw", 0, 144), R("iot", 0, 144), gc15, A.is_equal, col("nuf"), A.mult)
    ts(R("z1", 0, 144), R("iot", 0, 144), gc15, A.is_equal)
    ts(full("nii"), full("nxi"), 15, A.bitwise_and)
    ts(full("nci"), full("nxi"), 4, A.arith_shift_right)
    ts(full("p1"), full("nxi"), 0.5 - NP, A.add, 8192.0, A.mult)
    ts(full("p0"), full("nii"), float(RS), A.mult)
    tt(full("t2"), full("p1"), full("nxi"), A.min)
    tt(R("p0", RS, 2 * RS), full("p0"), full("nci"), A.add)
    ts(full("t1"), full("nxi"), float(NP), A.is_ge, float(NI), A.mult)
    tt(full("p2"), R("p0", RS, 2 * RS), full("t2"), A.max)
    cp("V", full("volw"), full("voli"))
    torow("st", IH, full("ohw"))
    torow("st", VO, full("volw"))
    ts(full("p3"), full("p2"), ROUND16, A.add, -ROUND16, A.add)
    cp("S", full("lab"), full("p2"))
    tt(R("m34", 0, 128), R("z1", 15 - CH, 143 - CH), R("z1", 15 - CL, 143 - CL), A.add)
    cp("S", full("hi"), full("p3"))
    tt(full("lo"), full("p3"), full("lab"), A.subtract)
    tt(full("hx"), full("p3"), full("t1"), A.add)
    shifted(full("olw"), full("olw"), pm)
    torow("st", IL, full("olw"))
    ts(wt(2), oh(HI), oh(IH), A.add)
    ts(wt(3), oh(IL), oh(LO), A.subtract)
    ts(sq("dg", 0), R("iot", 0, 128), pc, A.is_equal)
    h = RS // XQ
    for u in range(XQ):
        unwrap16(R("p5", h * u, h * u + h), "zw", R("pool", qx * u, qx * u + qx))
    cp("S", full("mh"), full("p5"))
    torow("st", CH, full("mh"), "S")
    tt(full("t2"), full("p2"), full("t1"), A.add)
    tt(full("ml"), full("p5"), full("mh"), A.subtract)
    torow("st", CL, full("ml"))
    for row, src in ((HI, "hi"), (LO, "lo"), (HX, "hx"), (VO, "volw")):
        torow("kw", row, full(src))
    for k in (1, 2):
        scaled(sq("dg", k), sq("dg", 0), wt(k + 1))
    scaled(sq("we", 4), R("m34", 0, 128), col("nuf"))
    ts(R("bi", 0, 18), R("iot", 0, 18), -float(NI), A.mult, wt(2), A.mult)
    ts(wt(5), oh(CH), oh(CL), A.add)
    ts(wt(4), oh(DH), oh(DL), A.add, oh(LO), A.subtract)
    ts(wt(7), oh(P0), oh(P1), A.add, oh(P2), A.add)
    ts(gi, gc15, -15.0, A.add, 1.0 / 16, A.mult)
    ts(wt(6), wt(4), oh(HI), A.add)
    cp("V", R("nxe", RS, 2 * RS), full("t2"))
    ts(R("pat", 0, 128), R("pat", 0, 128), gi, A.is_equal)
    ts(wt(1), oh(G0), oh(G1), A.add, oh(G2), A.add)
    ts(wt(9), pm, PL - 1.5, A.is_lt, 128.0, A.mult)
    ts(wt(10), oh(IH), oh(IL), A.add)
    ts(wt(8), wt(1), -1.0, A.mult)
    rows("p7", [], [], None, R("st", NP, NW), 12)
    dma("Y", T.kw[:, NP:NW], T.st[:, NP:NW], [R("st", NP, NW)], [R("kw", NP, NW)])
    rows("p6", [(0, NI, ap(sq("we", 4)), T.pool[:, 0:NI])], [R("pool", 0, NI), sq("we", 4)], "tba", blk("vw", 1), 0)
    ts(wt(0), oh(HX), oh(LO), A.subtract)
    tt(R("dl", 0, 16), R("lab", NC, NC + 16), R("lab", 0, 16), A.subtract)
    ts(R("base", 0, 16), R("iot", 0, 16), 16.0, A.mult, pm, A.add)
    ts(R("base", 16, 32), R("base", 0, 16), 1.0 / NI, A.mult)
    ts(R("fb", 0, 16), R("iot", 0, 16), 16.0, A.mult)
    ts(R("fb", 16, 32), R("iot", 0, 16), 16.0, A.mult, 128.0 * (PL - 1), A.add)
    ts(R("fb", 32, 48), R("iot", 0, 16), 0.0, A.mult, pm, A.add)
    ts(pr, pm, float(RS), A.mult)
    ts(R("qq", 0, 16), R("iot", 0, 16), pr, A.add)
    for s in range(4):
        add("V", (lambda s=s: g.vector.tensor_scalar(ap(sq("we", s)), T.m34[:, :], T.rcv[:, s, 64:65], None, A.mult)),
            [R("m34"), R("rcv")], [sq("we", s)], 64 * CY)
    selector("zmu", wt(5))
    selector("zvol", oh(VO))
    rows("p7", [(64 * s, 64 * s + 64, ap(sq("we", s)), T.rcv[:, s, 0:64]) for s in range(4)], [R("rcv"), R("we", 0, 512)], "tbe",
         R("st", NW, NW + NI), None)
    scaled(sq("bw", 0), R("pat", 0, 128), wt(7))
    scaled(sq("bw", 1), R("pat", 0, 128), wt(8))
    send(0, [T.pool[:, NP + 64 * s:NP + 64 * s + 64] for s in range(4)], [T.pool[:, NW + 64 * s:NW + 64 * s + 64] for s in range(4)],
         up, [R("pool", NP, NW), R("st", 0, NP, [CL])], [R("pool", NW, NW + NI)])
    for k in range(1, PL):
        select(sq("zd", k), sq("bw", 0), [[0, 8], [-1, 16]], k - 1)
    select(R("zc", 0, 128), R("pat", 0, 128), [[-16, 8], [-3, 16]], -3, 1)
    tt(full("dab"), full("lei"), R("lei", RS, 2 * RS), A.subtract)
    cp("V", R("lagr", 0, 16), R("lagi", 0, 16))
    cp("V", R("ohw", 0, 16), R("lagi", 0, 16))
    tt(ha("d4"), hb("hi"), ha("hi"), A.subtract)
    tt(R("lagr", 16, 32), R("lagr", 0, 16), R("ohw", 0, 16), A.subtract)
    tt(ha("d4", RS), ha("lo"), hb("lo"), A.subtract)
    cp("V", R("volw", 0, 16), R("lagr", 16, 32))
    ts(hb("d4"), ha("d4"), -1.0, A.mult)
    ts(hb("d4", RS), ha("d4", RS), -1.0, A.mult)
    tt(ha("dd"), hb("dab"), ha("dab"), A.subtract)
    tt(R("olw", 0, 16), R("lagr", 16, 32), R("volw", 0, 16), A.subtract)
    for row, src in ((G0, "ohw"), (G1, "volw"), (G2, "olw")):
        torow("kw", row, full(src))
    ts(wt(11), pc, 16.0, A.add)
    ts(wt(12), pm, 2.5, A.is_lt)
    ts(R("dp", 0, 160), R("iot", 0, 160), wt(11), A.is_equal, wt(7), A.mult)
    ts(R("dp", 160, 320), R("iot", 0, 160), wt(11), A.is_equal, wt(8), A.mult)
    scaled(sq("bw", 2), R("pat", 0, 128), wt(12))
    selector("zn", wt(6))
    selector("zf", wt(9))
    selector("zo", wt(10))
    selector("zx", wt(0))
    tt(sq("zd", 1), sq("zd", 1), sq("bw", 1), A.add)
    tt(R("zc", 0, 128), R("zc", 0, 128), sq("bw", 2), A.add)

    Q = lambda k, lo=0, hi=16: R("qq", 32 * k + lo, 32 * k + hi)
    F = lambda k: R("qq", 32 * k + 48, 32 * k + 64)
    OF = R("qq", 32 * (PL + 2), 32 * (PL + 2) + 16)
    entry = lambda i: blk("vw", i) if i > 1 else blk("b0", 0)
    dbank = lambda k: ("p4", "p5", "p7")[k % 3]

    def walk(k):
        if k <= SHARE:
            gather("V", R("vw", NI * k, NI * k + 128), R("kw", 0, NW), Q(k - 1, 0, 8))
            gather("S", R("vw", NI * k + 128, NI * k + NI), R("kw", 0, NW), Q(k - 1, 8, 16))
        else:
            gather("S", blk("vw", k), R("kw", 0, NW), Q(k - 1))

    def move(k):
        gather("S", blk("vg", k - 1), R("vw", 0, NI * (k + 1)), F(k))

    def scatter(k):
        add("V", lambda: g.vector.tensor_copy(T.st[:, 0:NW].indirect(ap(Q(k))), ap(blk("vg", k - 1))),
            [blk("vg", k - 1), Q(k)], [R("st", 0, NW)], 50 + NI * SC * CY)

    done = {}

    def dsum(k, upto, most=PL):
        if k > KEEP + 1:
            terms = [(0, R("zc", 0, 128), blk("ck", 0))] + [(i, sq("zd", i), entry(i)) for i in range(KEEP + 1, k + 1)]
        else:
            terms = [(i, sq("zd", i), entry(i)) for i in range(1, k + 1)]
        lo = done.get(k, 0)
        idx = [i for i in range(lo, len(terms)) if terms[i][0] <= upto][:most]
        done[k] = lo + len(idx)
        if idx:
            mm([(T[dbank(k)][:, 0:NI], ap(terms[i][1]), ap(terms[i][2]), i == 0, i == len(terms) - 1) for i in idx],
               [r for i in idx for r in terms[i][1:]], [R(dbank(k), 0, NI)])
        return len(idx)

    def sign(k):
        o = R(dbank(k), 0, NI)
        if k <= VSIGN:
            ts(blk("sg", k - 1), o, 0.0, A.is_ge, 2.0, A.mult)
        else:
            shifted(blk("sg", k - 1), o, half, SIGN)

    def keep(i):
        it = [T.dp[:, 176 + G0:304 + G0]] if i == 1 else []
        it += [T.dp[:, 16 + P0 - 3 * i:144 + P0 - 3 * i]]
        mm([(T.p6[:, 0:NI], l, ap(entry(i)), i == 1 and x == 0, i == KEEP) for x, l in enumerate(it)], [R("dp"), entry(i)], [R("p6", 0, NI)])

    def kept(k):
        if k == KEEP:
            cp("S", blk("ck", 0), R("p6", 0, NI))

    fbank = lambda k: R("p%d" % (2 + k % 2), 0, 16) if k in APART else R("p%d" % ((k + 1) % 2), 16, 32)

    def foot(k):
        unwrap16(fbank(k), "zf", blk("sg", k - 1), [R("fb", 0, 16) if k <= VSIGN else R("fb", 16, 32), R("fb", 32, 48)])

    fixed[0] = True
    for t in range(NR):
        last = t == NR - 1
        alo, so = NW + NI * t, NI * (t - 1)
        sold, sn = R("p5", 384 - NC * (t % 2), 480 - NC * (t % 2)), R("p5", 288 + NC * (t % 2), 384 + NC * (t % 2))
        dma("Y", T.kw[3:128:4, 0:NP], T.st[3:128:4, 0:NP], [R("st", 0, NP, range(3, 16, 4))], [R("kw", 0, NP, range(3, 16, 4))])
        if t == 0:
            for x, (e, lo, hi) in enumerate(XCH0):
                gather(e, R("gx", 16 * lo, 16 * hi), R("st", 0, NW + NI), R("nxe", RS + lo, RS + hi))
                if x % 2:
                    for bank, z in (("p5", "zmu"), ("p4", "zvol")):
                        unwrap16(R(bank, hi - 64, hi), z, R("gx", 16 * hi - 1024, 16 * hi))
            cp("S", full("voln"), full("p4"))
        else:
            unwrap16(R("p0", 0, 16), "zo", R("st", NP, NW))
            for x, (e, lo, hi) in enumerate(XCH):
                gather(e, R("gx", 16 * lo, 16 * hi), R("st", 0, NW + NI), R("nxe", lo, hi))
                if x == 0:
                    cp("V", OF, R("p0", 0, 16))
                if x == 1:
                    gather("S", R("snd", so, so + NI), R("pool", 0, alo), OF)
                    send(t, [T.snd[:, so + 64 * s:so + 64 * s + 64] for s in range(4)],
                         [T.pool[:, alo + 64 * s:alo + 64 * s + 64] for s in range(4)], up, [R("snd", so, so + NI)], [R("pool", alo, alo + NI)])
                j0, j1 = lo // 12, hi // 12
                if j0 < j1:
                    unwrap(full("p5"), "zmu", R("gx", RS * j0, RS * j1), lambda j: T.gx[:, RS * j:RS * j + RS], j0, j1)
            cp("S", blk("vw", 1), blk("vw", 0))
        co = "dab" if t == 0 else "ab"
        tt(ha("xa"), ha("p5"), ha(co), A.mult)
        tt(ha("p5", RS), hb("p5"), hb(co), A.mult)
        tt(ha("cn"), ha("p5"), ha("voln"), A.mult)
        tt(ha("p1"), hb("p5"), hb("voln"), A.mult)
        tt(ha("df"), ha("p5", RS), ha("xa"), A.subtract)
        tt(ha("dcn"), ha("p1"), ha("cn"), A.subtract)
        if t > 0:
            tt(sn, ha("df"), sold, A.is_lt)
        else:
            ts(sn, ha("df"), 0.0, A.is_lt)
        tt(ha("ee"), sn, ha("dcn"), A.mult)
        for x, row in enumerate((DH, DL)):
            tt(ha("dy", RS * x), sn, ha("d4", RS * x), A.mult)
            tt(hb("dy", RS * x), sn, hb("d4", RS * x), A.mult)
            torow("kw", row, R("dy", RS * x, RS * x + RS))
        tt(hb("pp"), ha("p1"), ha("ee"), A.subtract)
        tt(ha("pp"), ha("ee"), ha("cn"), A.add)
        tt(R("q1", 0, 16), R("p5", sn[2], sn[2] + 16), R("dl", 0, 16), A.mult)
        cp("S", full("c0"), full("pp"))
        torow("kw", P0, full("c0"), "S")
        ts(full("p1"), full("pp"), ROUND128, A.add, -ROUND128, A.add)
        tt(R("q1", 16, 32), R("q1", 0, 16), R("lab", 0, 16), A.add)
        tt(R("q1", 32, 48), R("pp", 0, 16), R("lagr", 0, 16), A.is_ge)
        tt(full("c2"), full("pp"), full("p1"), A.subtract)
        torow("kw", P2, full("c2"))
        tt(full("c1"), full("p1"), full("c0"), A.subtract)
        torow("kw", P1, full("c1"))
        cp("V", Q(1), R("q1", 16, 32))
        tt(R("q1", 48, 64), R("q1", 32, 48), R("base", 16, 32), A.add)
        if last:
            tt(ha("dn"), hb("nxi"), ha("nxi"), A.subtract)
        step, old, new = ("dn", "nxi", "ynb") if last else ("dd", "dab", "ab")
        tt(ha("p5", RS), sn, ha(step), A.mult)
        ts(F(1), R("q1", 48, 64), float(NI), A.mult)
        rows("p6", [(0, NI, ap(sq("we", 4)), T.pool[:, alo:alo + NI])], [R("pool", alo, alo + NI), sq("we", 4)], "tba", blk("vw", 0), 13 + t)
        tt(ha(new), ha("p5", RS), ha(old), A.add)
        tt(hb(new), hb(old), ha("p5", RS), A.subtract)
        if last:
            dma("Y", T.yn[:, :], T.ynb[:, :], [R("ynb")], [])
            dma("Y", T.y[:, 0:NI], T.pool[:, alo:alo + NI], [R("pool", alo, alo + NI)], [])
        else:
            sb, sr = ("snd", so) if t > 0 else ("pool", NP)
            rows("p3", [(64 * s, 64 * s + 64, ap(sq("we", s)), T[sb][:, sr + 64 * s:sr + 64 * s + 64]) for s in range(4)],
                 [R(sb, sr, sr + NI), R("we", 0, 512)], "tbe", R("st", NW, NW + NI), None)
        move(1)
        done.clear()
        for k in range(2, PL):
            bank = "p%d" % (k % 2)
            wide = 16 if k == 2 or k - 1 in APART else 32

            def ahead(k):
                used = dsum(k + 1, k)
                if KEEP < k < PL - 2:
                    dsum(k + 2, k, max(0, AHEAD - used))

            calls = {"g": walk, "b": lambda k: gather("S", blk("b0", 0), R("kw", 0, NW), Q(0)),
                     "n": lambda k: unwrap16(R(bank, 0, 16), "zn", blk("vw", k)), "q": lambda k: cp("V", Q(k, 0, wide), R(bank, 0, wide)),
                     "d": lambda e: dsum(e, k), "a": ahead, "k": keep, "c": kept, "s": sign, "f": foot,
                     "o": lambda k: cp("V", F(k), fbank(k)), "m": move, "w": scatter}
            for x in STEP.get(k, STEP[0]).split():
                calls[x[0]](k - int(x[1:] or 0))
            if t == 0 and 6 <= k < 10:
                unwrap(full("p6"), "zx", R("kw", 0, NP), lambda j: T.kw[:, j:NP:16], 4 * k - 24, 4 * k - 20)
            if t == 0 and k == 10:
                cp("V", full("nxe"), full("p6"))
    for bank, lo, hi in (("p5", 0, 64), ("p6", 64, 128), ("p7", 128, 176)):
        unwrap(R(bank, 0, hi - lo), "zo", R("st", 0, NP), lambda j, lo=lo, hi=hi: T.st[:, RS * j + 16 + lo:RS * j + 16 + hi])
    unwrap16(R("p7", 48, 64), "zo", R("st", NP, NW))
    for x, (e, lo, hi) in enumerate(YCH):
        if x % 2 == 0:
            cp("V", R("ofy", lo, lo + 64), R(("p5", "p6", "p7")[x // 2], 0, 64))
        gather(e, R("gx", 16 * lo, 16 * hi), R("pool", 0, NW + NR * NI), R("ofy", lo, hi))
        dma("Y", T.y[:, NI + 16 * lo:NI + 16 * hi], T.gx[:, 16 * lo:16 * hi], [R("gx", 16 * lo, 16 * hi)], [])
    return ops, q, nrl[0]


def depend(ops):
    dep = [set() for _ in ops]
    hist = {}
    for i, o in enumerate(ops):
        for kind, regs in (("r", o["rd"]), ("w", o["wr"]), ("x", o["ex"])):
            for r in regs:
                for j, k2, r2 in hist.get(r[0], []):
                    if overlap(r, r2) and ((kind == "r" and k2 == "w") or (kind == "w" and k2 != "x")
                                           or (kind == "x" and k2 == "x" and (ops[j]["eng"] != o["eng"] or o["eng"] == "P"))):
                        dep[i].add(j)
        for kind, regs in (("r", o["rd"]), ("w", o["wr"]), ("x", o["ex"])):
            for r in regs:
                hist.setdefault(r[0], []).append((i, kind, r))
        if o["kind"] == "a":
            dep[i].add(i - 1)
    return dep


def order(ops, dep):
    n = len(ops)
    dep = [set(d) for d in dep]
    tail, chain = {}, set()
    for i, o in enumerate(ops):
        if o["fixed"] and o["eng"] is not None:
            if o["eng"] in tail and tail[o["eng"]] not in dep[i]:
                dep[i].add(tail[o["eng"]])
                chain.add((tail[o["eng"]], i))
            tail[o["eng"]] = i
    gap = lambda j, i: -ops[j]["lat"] if (j, i) in chain else 0.0 if ops[j]["eng"] == ops[i]["eng"] == "P" else WAKE
    prio = [0.0] * n
    for i in range(n - 1, -1, -1):
        prio[i] += ops[i]["dur"] + ops[i]["lat"]
        for j in dep[i]:
            prio[j] = max(prio[j], prio[i] + gap(j, i) + 0.01)
    start, fin = [0.0] * n, [0.0] * n
    busy = {e: [] for e in ("V", "S", "P", "G", "Y")}
    for i in sorted(range(n), key=lambda i: (-prio[i], i)):
        t = max([fin[j] + gap(j, i) for j in dep[i]] + [0.0])
        e, d = ops[i]["eng"], ops[i]["dur"]
        if e is not None:
            l = busy[e]
            k = len(l)
            while k > 0 and l[k - 1][1] > t:
                k -= 1
            while k < len(l) and l[k][0] < t + d:
                t = max(t, l[k][1])
                k += 1
            l.insert(k, (t, t + d))
        start[i] = t
        fin[i] = t + d + ops[i]["lat"]
    return sorted(range(n), key=lambda i: (start[i], i))


def rank_program(g, core, T, topo):
    if T.rank_of(core) is None:
        return
    ops, q, nrl = build(g, core, T, topo)
    dep = depend(ops)
    seq = order(ops, dep)
    pos = {i: k for k, i in enumerate(seq)}
    seen, marked = {}, set()
    waits = [[] for _ in ops]
    for i in seq:
        o = ops[i]
        if o["kind"] == "a":
            continue
        need = {}
        for j in dep[i]:
            p = ops[j]
            if p["kind"] == "r" or (p["eng"] == "P" and o["eng"] == "P"):
                continue
            key = (o["eng"], p["eng"] if p["kind"] == "c" else p["tok"][0])
            if key not in need or pos[j] > pos[need[key]]:
                need[key] = j
        for key, j in sorted(need.items(), key=lambda kj: pos[kj[1]]):
            if seen.get(key, -1) < pos[j]:
                seen[key] = pos[j]
                waits[i].append(j)
                marked.add(j)
    count = {}
    for i in seq:
        o = ops[i]
        if o["kind"] == "c" and i in marked:
            s = "c" + o["eng"]
            count[s] = count.get(s, 0) + 1
            o["tok"] = (s, count[s])
    for i in seq:
        o = ops[i]
        if o["kind"] == "a":
            continue
        for j in waits[i]:
            q[o["eng"]].wait_ge(T.sem[ops[j]["tok"][0]], ops[j]["tok"][1])
        ins = o["fn"]()
        if o["kind"] == "d":
            ins.then_inc(T.sem[o["tok"][0]], 16)
        elif o["kind"] == "c" and i in marked:
            ins.then_inc(T.sem[o["tok"][0]], 1)
    g.wait_ge(T.sem.rl, nrl)
    for i in seq:
        if ops[i]["kind"] in "da" and i not in marked:
            g.wait_ge(T.sem[ops[i]["tok"][0]], ops[i]["tok"][1])
